import numpy as np
import ml_dtypes


def mxq(x, axis, fmt="e4m3"):
    dtype, down = {"e4m3": (ml_dtypes.float8_e4m3fn, 7), "e5m2": (ml_dtypes.float8_e5m2, 14)}[fmt]
    v = np.moveaxis(np.asarray(x, np.float32).astype(ml_dtypes.bfloat16).astype(np.float64), axis, -1)
    blocks = v.reshape(v.shape[:-1] + (-1, 32))
    amax = np.abs(blocks).max(-1, keepdims=True)
    byte = np.maximum(np.where(amax > 0, np.frexp(amax)[1] - 1 + 127, 0) - down, 1)
    scale = np.exp2(byte - 127.0)
    codes = (blocks / scale).astype(np.float32).astype(dtype).astype(np.float64)
    return np.moveaxis((codes * scale).reshape(v.shape), -1, axis)


WIDE = False


def mx_kscale(k):
    if not WIDE:
        return np.ones(k)
    levels = np.array([10, -10, 5, -5, 0])
    if k % 512:
        return np.exp2(np.random.permutation(np.resize(levels, k // 32))).repeat(32)
    a = np.empty((k // 512, 16))
    for p in range(k // 512):
        a[p, :8] = np.random.permutation(np.resize(levels, 8))
        for g in range(8):
            far = levels[np.abs(levels - a[p, g]) >= 10]
            a[p, g + 8] = far[np.random.randint(len(far))]
    return np.exp2(a.ravel()).repeat(32)


def f64(x):
    return np.asarray(x).astype(np.float64)


def striped(idx):
    return np.tile(idx.reshape(-1, 16).T, (8, 1)).astype(np.uint16)


def unstriped(offs):
    return offs[:16].T.reshape(-1).astype(np.int64)


E2M1 = np.array([0.0, 0.5, 1.0, 1.5, 2.0, 3.0, 4.0, 6.0, -0.0, -0.5, -1.0, -1.5, -2.0, -3.0, -4.0, -6.0])


def pack_weight(w, fmt):
    k, n = w.shape
    w = f64(np.asarray(w, np.float32).astype(ml_dtypes.bfloat16)).reshape(k // 32, 32, n)
    amax = np.abs(w).max(1)
    if fmt == "e4m3":
        byte = np.frexp(amax)[1] - 1 + 127 - 7
    else:
        mant, ex = np.frexp(amax / 6.0)
        byte = np.where(mant > 0.5, ex, ex - 1) + 127
    byte = np.clip(np.where(amax > 0, byte, 1), 1, 254)
    scaled = (w * np.exp2(127.0 - byte)[:, None, :]).reshape(k, n).astype(np.float32)
    by_word = np.ascontiguousarray(scaled.reshape(k // 512, 128, 4, n).transpose(0, 1, 3, 2))
    if fmt == "e4m3":
        words = by_word.astype(ml_dtypes.float8_e4m3fn).view(np.uint8)
    else:
        c = by_word.astype(ml_dtypes.float4_e2m1fn).view(np.uint8) & 0xF
        words = (c[..., 0::2] | (c[..., 1::2] << 4)).reshape(k // 512, 128, 2 * n)
    return np.ascontiguousarray(words), np.ascontiguousarray(byte.astype(np.uint8).reshape(k // 512, 16, n))


def unpack_weight(words, scales, fmt):
    g, _, n = scales.shape
    words = np.ascontiguousarray(words).reshape(g, 128, n, -1)
    if fmt == "e4m3":
        vals = words.view(ml_dtypes.float8_e4m3fn).astype(np.float64)
    else:
        nib = np.empty((g, 128, n, 4), np.uint8)
        nib[..., 0::2] = words & 0xF
        nib[..., 1::2] = words >> 4
        vals = E2M1[nib]
    vals = vals * np.repeat(np.exp2(scales.astype(np.float64) - 127.0), 8, axis=1)[..., None]
    return vals.transpose(0, 1, 3, 2).reshape(g * 512, n)


def planes(y):
    n, m = y.shape
    v = y.astype(np.float32).astype(ml_dtypes.bfloat16).astype(np.float64).reshape(n // 32, 32, m)
    top = np.abs(v).max(1)
    byte = np.clip(np.where(top > 0, np.frexp(top)[1] - 1 + 127 - 7, 1), 1, 254)
    codes = (v * np.exp2(127.0 - byte)[:, None, :]).reshape(n, m).astype(np.float32).astype(ml_dtypes.float8_e4m3fn).view(np.uint8)
    words = codes.reshape(n // 512, 128, 4, m).transpose(0, 1, 3, 2)
    return np.ascontiguousarray(words), np.ascontiguousarray(byte.astype(np.uint8).reshape(n // 512, 16, m))


K, T, E, G, H, N = 512, 256, 6, 3, 512, 512


def setup_inputs():
    n = np.random.standard_normal
    s = mx_kscale(K)
    u = mx_kscale(H)
    chosen = np.random.permutation(E)[:G]
    x = pack_weight(n((K, T)) * s[:, None], "e4m3")
    w1 = pack_weight(n((K, E * H)) / np.sqrt(K) / s[:, None] * np.tile(u, E), "e4m3")
    w2 = pack_weight(n((H, E * N)) / np.sqrt(H) / u[:, None], "e4m3")
    return {
        "x_words": x[0],
        "x_scales": x[1],
        "w1_words": w1[0],
        "w1_scales": w1[1],
        "w2_words": w2[0],
        "w2_scales": w2[1],
        "gate": np.stack([np.tile(r, (128, 1)) for r in np.random.uniform(0.2, 1.0, (G, T))]).astype(np.float32),
        "offs": striped((chosen[:, None] * H + np.arange(H)).reshape(-1)),
        "offs2": striped((chosen[:, None] * N + np.arange(N)).reshape(-1)),
    }


def reference(x_words, x_scales, w1_words, w1_scales, w2_words, w2_scales, gate, offs, offs2):
    idx, idx2 = unstriped(offs), unstriped(offs2)
    x = unpack_weight(x_words, x_scales, "e4m3")
    w1 = unpack_weight(w1_words, w1_scales, "e4m3")[:, idx]
    w2 = unpack_weight(w2_words, w2_scales, "e4m3")[:, idx2]
    y = np.zeros((N, T))
    for r in range(G):
        h = f64(gate[r, :1]) * (w1[:, r * H:(r + 1) * H].T @ x)
        y = y + w2[:, r * N:(r + 1) * N].T @ mxq(h, 0, "e4m3")
    out_0 = y
    return (out_0,) + planes(out_0)

@@ -1,0 +1,175 @@
+from contextlib import ExitStack
+
+import concourse.mybir as mybir
+from concourse.masks import make_identity
+
+F32 = mybir.dt.float32
+BF16 = mybir.dt.bfloat16
+I32 = mybir.dt.int32
+U32 = mybir.dt.uint32
+U16 = mybir.dt.uint16
+U8 = mybir.dt.uint8
+FP8X4 = mybir.dt.float8_e4m3fn_x4
+COPY = mybir.ActivationFunctionType.Copy
+
+P = 128
+T = 256
+G = 3
+WIDTH = 512
+COLUMNS = 3072
+HALVES = T // P
+PER_COLUMN = 16
+GATE_STEP = 5
+
+FLOPS = 2 * 2 * G * WIDTH * WIDTH * T
+
+
+def load_scale_rows(nc, plane, scales):
+    rows = scales[0].bitcast(I32).rearrange("(q v) c -> q (v c)", v=4)
+    for q in range(4):
+        nc.sync.dma_start(out=plane[32 * q : 32 * (q + 1), :].bitcast(I32), in_=rows[q].partition_broadcast(8))
+
+
+def load_words(nc, tile, words):
+    nc.sync.dma_start(out=tile[:].bitcast(I32), in_=words[0].rearrange("p m d -> p (m d)").bitcast(I32))
+
+
+def tile_moe_wsel_b_none_p_kernel(
+    tc, x_words, x_scales, w1_words, w1_scales, w2_words, w2_scales, gate, offs, offs2, out_0, out_1, out_2
+):
+    nc = tc.nc
+    with ExitStack() as ctx:
+        held = ctx.enter_context(tc.tile_pool(name="held", bufs=1))
+        psum = ctx.enter_context(tc.psum_pool(name="psum", bufs=1))
+
+        list1 = held.tile([P, G * WIDTH // PER_COLUMN], U16, name="list1")
+        list2 = held.tile([P, G * WIDTH // PER_COLUMN], U16, name="list2")
+        w1_all = held.tile([P, COLUMNS], U32, name="w1_all", align_bytes=64)
+        w2_all = held.tile([P, COLUMNS], U32, name="w2_all", align_bytes=64)
+        s1_all = held.tile([P, COLUMNS], U8, name="s1_all", align_bytes=64)
+        s2_all = held.tile([P, COLUMNS], U8, name="s2_all", tag="after_s2", align_bytes=64)
+        x_codes = held.tile([P, T], U32, name="x_codes", align_bytes=64)
+        x_plane = held.tile([P, T], U8, name="x_plane", align_bytes=64)
+        gate_rows = held.tile([P, P], F32, name="gate_rows")
+        gate_cols = held.tile([P, P], F32, name="gate_cols")
+        identity = held.tile([P, P], F32, name="identity")
+
+        make_identity(nc, identity[:])
+
+        nc.sync.dma_start(list1[:], offs)
+        load_scale_rows(nc, s1_all, w1_scales)
+        nc.sync.dma_start(
+            out=gate_rows[:],
+            in_=gate.rearrange("r p (j t) -> (r p j) t", j=HALVES)[0 : GATE_STEP * P : GATE_STEP, :],
+        )
+        load_words(nc, x_codes, x_words)
+        load_words(nc, w1_all, w1_words)
+        nc.sync.dma_start(list2[:], offs2)
+        load_scale_rows(nc, x_plane, x_scales)
+        load_scale_rows(nc, s2_all, w2_scales)
+        load_words(nc, w2_all, w2_words)
+
+        gate_bank = psum.tile([P, P], F32, name="gate_bank", tag="sums", bufs=3)
+        nc.tensor.transpose(gate_bank[:], gate_rows[:], identity[:])
+        nc.scalar.activation(out=gate_cols[:], in_=gate_bank[:], func=COPY)
+
+        def gate_column(r, j):
+            a = 2 * -(-r * P * HALVES // (2 * GATE_STEP)) + j
+            return gate_cols[:, a : a + 1]
+
+        per_expert = WIDTH // PER_COLUMN
+        s1 = held.tile([P, G * WIDTH], U8, name="s1", align_bytes=64)
+        nc.vector.tensor_copy(out=s1[:], in_=s1_all[:].indirect(list1[:]))
+        w1 = []
+        for r in range(G):
+            w1.append(held.tile([P, WIDTH], U32, name="w1_%d" % r, align_bytes=64))
+            nc.vector.tensor_copy(
+                out=w1[r][:], in_=w1_all[:].indirect(list1[:, r * per_expert : (r + 1) * per_expert])
+            )
+        s2 = held.tile([P, G * WIDTH], U8, name="s2", align_bytes=64)
+        nc.vector.tensor_copy(out=s2[:], in_=s2_all[:].indirect(list2[:]))
+
+        h_grouped = []
+        for r in range(G):
+            turned = psum.tile([P, HALVES, 2, P], F32, name="turned", tag="turned", bufs=2)
+            for j in range(HALVES):
+                tokens = slice(j * P, (j + 1) * P)
+                sums = psum.tile([P, WIDTH], F32, name="sums", tag="sums", bufs=3)
+                nc.tensor.matmul_mx(
+                    out=sums[:],
+                    lhsT=x_codes[:, tokens].bitcast(FP8X4),
+                    lhsT_scale=x_plane[:, tokens],
+                    rhs=w1[r][:].bitcast(FP8X4),
+                    rhs_scale=s1[:, r * WIDTH : (r + 1) * WIDTH],
+                    start=True,
+                    stop=True,
+                )
+                h_rows = held.tile([P, 2, P, 2], BF16, name="h_rows_%d_%d" % (r, j))
+                nc.scalar.activation(
+                    out=h_rows[:],
+                    in_=sums[:].rearrange("t (p u e) -> t u p e", u=2, e=2),
+                    func=COPY,
+                    scale=gate_column(r, j),
+                )
+                pairs = h_rows[:].rearrange("t u p e -> t (u p e)").bitcast(F32)
+                for u in range(2):
+                    nc.tensor.transpose(turned[:, j, u, :], pairs[:, u * P : (u + 1) * P], identity[:])
+            h_grouped.append(held.tile([P, T * 4], BF16, name="h_grouped_%d" % r, align_bytes=64))
+            nc.scalar.copy(
+                out=h_grouped[r][:].bitcast(F32).rearrange("p (j t u) -> p j t u", j=HALVES, u=2),
+                in_=turned[:].rearrange("p j u t -> p j t u"),
+            )
+
+        y_sums = [psum.tile([P, WIDTH], F32, name="y_sums_%d" % j) for j in range(HALVES)]
+        keep = []
+        for r in range(G):
+            h_codes = held.tile([P, T], U32, name="h_codes_%d" % r, tag="after_s2" if r == 0 else "h_codes_%d" % r, align_bytes=64)
+            h_plane = held.tile([P, T], U8, name="h_plane_%d" % r, align_bytes=64)
+            nc.vector.quantize_mx(out=h_codes[:].bitcast(FP8X4), scales=h_plane[:], in_=h_grouped[r][:])
+            w2 = held.tile([P, WIDTH], U32, name="w2_%d" % r, align_bytes=64)
+            nc.vector.tensor_copy(
+                out=w2[:], in_=w2_all[:].indirect(list2[:, r * per_expert : (r + 1) * per_expert])
+            )
+            keep.append((h_codes, w2))
+            for j in range(HALVES):
+                tokens = slice(j * P, (j + 1) * P)
+                nc.tensor.matmul_mx(
+                    out=y_sums[j][:],
+                    lhsT=h_codes[:, tokens].bitcast(FP8X4),
+                    lhsT_scale=h_plane[:, tokens],
+                    rhs=w2[:].bitcast(FP8X4),
+                    rhs_scale=s2[:, r * WIDTH : (r + 1) * WIDTH],
+                    start=(r == 0),
+                    stop=(r == G - 1),
+                )
+
+        y_grouped = held.tile([P, T, 4], BF16, name="y_grouped", align_bytes=64)
+        out_rows = out_0.rearrange("(p d) t -> p d t", d=4)
+        for j in range(HALVES):
+            tokens = slice(j * P, (j + 1) * P)
+            y_rows = held.tile([P, 4, P], F32, name="y_rows_%d" % j)
+            dealt = y_sums[j][:].rearrange("t (p d) -> t d p", d=4)
+            if j == 0:
+                nc.scalar.copy(out=y_rows[:], in_=dealt)
+            else:
+                nc.vector.tensor_copy(out=y_rows[:], in_=dealt)
+            y_turned = psum.tile([P, 4, P], F32, name="y_turned", tag="sums", bufs=3)
+            for d in range(4):
+                nc.tensor.transpose(y_turned[:, d, :], y_rows[:, d, :], identity[:])
+            y = held.tile([P, 4, P], F32, name="y_%d" % j)
+            nc.scalar.copy(out=y[:], in_=y_turned[:])
+            nc.sync.dma_start(out=out_rows[:, :, tokens], in_=y[:])
+            nc.vector.tensor_copy(out=y_grouped[:, tokens, :], in_=y[:].rearrange("p d t -> p t d"))
+
+        y_codes = held.tile([P, T], U32, name="y_codes", align_bytes=64)
+        y_plane = held.tile([P, T], U8, name="y_plane", align_bytes=64)
+        nc.vector.quantize_mx(
+            out=y_codes[:].bitcast(FP8X4), scales=y_plane[:], in_=y_grouped[:].rearrange("p t d -> p (t d)")
+        )
+        nc.sync.dma_start(
+            out=out_1[0].rearrange("p t d -> p (t d)").bitcast(I32), in_=y_codes[:].bitcast(I32)
+        )
+        scale_rows = out_2[0].bitcast(I32)
+        for v in range(4):
+            queue = nc.scalar if v < 2 else nc.sync
+            queue.dma_start(out=scale_rows[v:16:4, :], in_=y_plane[v:P:32, :].bitcast(I32))

@@ -19,15 +19,20 @@ WIDTH = 512
 COLUMNS = 3072
 HALVES = T // P
 PER_COLUMN = 16
+X_ROW, W1_ROW, W2_ROW = 8, 0, 4
 GATE_STEP = 5
+W1_ALL_AT = 0
+S2_ALL_AT = W1_ALL_AT + 4 * COLUMNS
+W2_ALL_AT = S2_ALL_AT + COLUMNS
+ZEROS_AT = S2_ALL_AT - 128
 
 FLOPS = 2 * 2 * G * WIDTH * WIDTH * T
 
 
-def load_scale_rows(nc, plane, scales):
-    rows = scales[0].bitcast(I32).rearrange("(q v) c -> q (v c)", v=4)
-    for q in range(4):
-        nc.sync.dma_start(out=plane[32 * q : 32 * (q + 1), :].bitcast(I32), in_=rows[q].partition_broadcast(8))
+def load_scale_rows(nc, plane, scales, first_row):
+    rows = scales[0].bitcast(I32)
+    for v in range(4):
+        nc.sync.dma_start(out=plane[first_row + v : P : 32, :].bitcast(I32), in_=rows[v:16:4, :])
 
 
 def load_words(nc, tile, words):
@@ -40,34 +45,41 @@ def tile_moe_wsel_b_none_p_kernel(
     nc = tc.nc
     with ExitStack() as ctx:
         held = ctx.enter_context(tc.tile_pool(name="held", bufs=1))
+        shared = ctx.enter_context(tc.tile_pool(name="shared", bufs=1))
         psum = ctx.enter_context(tc.psum_pool(name="psum", bufs=1))
 
         list1 = held.tile([P, G * WIDTH // PER_COLUMN], U16, name="list1")
         list2 = held.tile([P, G * WIDTH // PER_COLUMN], U16, name="list2")
-        w1_all = held.tile([P, COLUMNS], U32, name="w1_all", align_bytes=64)
-        w2_all = held.tile([P, COLUMNS], U32, name="w2_all", align_bytes=64)
-        s1_all = held.tile([P, COLUMNS], U8, name="s1_all", align_bytes=64)
-        s2_all = held.tile([P, COLUMNS], U8, name="s2_all", tag="after_s2", align_bytes=64)
         x_codes = held.tile([P, T], U32, name="x_codes", align_bytes=64)
-        x_plane = held.tile([P, T], U8, name="x_plane", align_bytes=64)
         gate_rows = held.tile([P, P], F32, name="gate_rows")
         gate_cols = held.tile([P, P], F32, name="gate_cols")
         identity = held.tile([P, P], F32, name="identity")
 
+        def placed(shape, dtype, name, offset):
+            return shared.tile(shape, dtype, name=name, offset=offset, align_bytes=64)
+
+        s1_all = placed([P, COLUMNS], U8, "s1_all", W2_ALL_AT)
+        zeros = placed([P, T], U8, "zeros", ZEROS_AT)
+        x_plane = held.tile([P, T], U8, name="x_plane", align_bytes=64)
+        nc.vector.memset(s1_all[:].bitcast(I32), 0)
+        nc.vector.memset(zeros[:].bitcast(I32), 0)
+        nc.vector.tensor_copy(out=x_plane[:].bitcast(I32), in_=zeros[:].bitcast(I32))
+        s2_all = placed([P, COLUMNS], U8, "s2_all", S2_ALL_AT)
+        nc.vector.memset(s2_all[:].bitcast(I32), 0)
         make_identity(nc, identity[:])
 
         nc.sync.dma_start(list1[:], offs)
-        load_scale_rows(nc, s1_all, w1_scales)
+        load_scale_rows(nc, s1_all, w1_scales, W1_ROW)
+        w1_all = placed([P, COLUMNS], U32, "w1_all", W1_ALL_AT)
+        load_words(nc, w1_all, w1_words)
+        load_words(nc, x_codes, x_words)
         nc.sync.dma_start(
             out=gate_rows[:],
             in_=gate.rearrange("r p (j t) -> (r p j) t", j=HALVES)[0 : GATE_STEP * P : GATE_STEP, :],
         )
-        load_words(nc, x_codes, x_words)
-        load_words(nc, w1_all, w1_words)
         nc.sync.dma_start(list2[:], offs2)
-        load_scale_rows(nc, x_plane, x_scales)
-        load_scale_rows(nc, s2_all, w2_scales)
-        load_words(nc, w2_all, w2_words)
+        load_scale_rows(nc, x_plane, x_scales, X_ROW)
+        load_scale_rows(nc, s2_all, w2_scales, W2_ROW)
 
         gate_bank = psum.tile([P, P], F32, name="gate_bank", tag="sums", bufs=3)
         nc.tensor.transpose(gate_bank[:], gate_rows[:], identity[:])
@@ -80,6 +92,8 @@ def tile_moe_wsel_b_none_p_kernel(
         per_expert = WIDTH // PER_COLUMN
         s1 = held.tile([P, G * WIDTH], U8, name="s1", align_bytes=64)
         nc.vector.tensor_copy(out=s1[:], in_=s1_all[:].indirect(list1[:]))
+        w2_all = placed([P, COLUMNS], U32, "w2_all", W2_ALL_AT)
+        load_words(nc, w2_all, w2_words)
         w1 = []
         for r in range(G):
             w1.append(held.tile([P, WIDTH], U32, name="w1_%d" % r, align_bytes=64))
@@ -98,9 +112,9 @@ def tile_moe_wsel_b_none_p_kernel(
                 nc.tensor.matmul_mx(
                     out=sums[:],
                     lhsT=x_codes[:, tokens].bitcast(FP8X4),
-                    lhsT_scale=x_plane[:, tokens],
+                    lhsT_scale=x_plane[X_ROW:P, tokens],
                     rhs=w1[r][:].bitcast(FP8X4),
-                    rhs_scale=s1[:, r * WIDTH : (r + 1) * WIDTH],
+                    rhs_scale=s1[W1_ROW:P, r * WIDTH : (r + 1) * WIDTH],
                     start=True,
                     stop=True,
                 )
@@ -123,8 +137,8 @@ def tile_moe_wsel_b_none_p_kernel(
         y_sums = [psum.tile([P, WIDTH], F32, name="y_sums_%d" % j) for j in range(HALVES)]
         keep = []
         for r in range(G):
-            h_codes = held.tile([P, T], U32, name="h_codes_%d" % r, tag="after_s2" if r == 0 else "h_codes_%d" % r, align_bytes=64)
-            h_plane = held.tile([P, T], U8, name="h_plane_%d" % r, align_bytes=64)
+            h_codes = placed([P, T], U32, "h_codes_%d" % r, S2_ALL_AT + 4 * T * r)
+            h_plane = held.tile([P, T], U8, name="h_plane", bufs=2, align_bytes=64)
             nc.vector.quantize_mx(out=h_codes[:].bitcast(FP8X4), scales=h_plane[:], in_=h_grouped[r][:])
             w2 = held.tile([P, WIDTH], U32, name="w2_%d" % r, align_bytes=64)
             nc.vector.tensor_copy(
@@ -138,7 +152,7 @@ def tile_moe_wsel_b_none_p_kernel(
                     lhsT=h_codes[:, tokens].bitcast(FP8X4),
                     lhsT_scale=h_plane[:, tokens],
                     rhs=w2[:].bitcast(FP8X4),
-                    rhs_scale=s2[:, r * WIDTH : (r + 1) * WIDTH],
+                    rhs_scale=s2[W2_ROW:P, r * WIDTH : (r + 1) * WIDTH],
                     start=(r == 0),
                     stop=(r == G - 1),
                 )
@@ -157,9 +171,12 @@ def tile_moe_wsel_b_none_p_kernel(
             for d in range(4):
                 nc.tensor.transpose(y_turned[:, d, :], y_rows[:, d, :], identity[:])
             y = held.tile([P, 4, P], F32, name="y_%d" % j)
+            if j == 1:
+                nc.vector.tensor_copy(out=y_grouped[:, tokens, :], in_=y_turned[:].rearrange("p d t -> p t d"))
             nc.scalar.copy(out=y[:], in_=y_turned[:])
             nc.sync.dma_start(out=out_rows[:, :, tokens], in_=y[:])
-            nc.vector.tensor_copy(out=y_grouped[:, tokens, :], in_=y[:].rearrange("p d t -> p t d"))
+            if j == 0:
+                nc.vector.tensor_copy(out=y_grouped[:, tokens, :], in_=y[:].rearrange("p d t -> p t d"))
 
         y_codes = held.tile([P, T], U32, name="y_codes", align_bytes=64)
         y_plane = held.tile([P, T], U8, name="y_plane", align_bytes=64)

@@ -11,6 +11,7 @@ U16 = mybir.dt.uint16
 U8 = mybir.dt.uint8
 FP8X4 = mybir.dt.float8_e4m3fn_x4
 COPY = mybir.ActivationFunctionType.Copy
+MULT = mybir.AluOpType.mult
 
 P = 128
 T = 256
@@ -21,10 +22,7 @@ HALVES = T // P
 PER_COLUMN = 16
 X_ROW, W1_ROW, W2_ROW = 8, 0, 4
 GATE_STEP = 5
-W1_ALL_AT = 0
-S2_ALL_AT = W1_ALL_AT + 4 * COLUMNS
-W2_ALL_AT = S2_ALL_AT + COLUMNS
-ZEROS_AT = S2_ALL_AT - 128
+VECTOR_EXPERT = 1
 
 FLOPS = 2 * 2 * G * WIDTH * WIDTH * T
 
@@ -54,34 +52,32 @@ def tile_moe_wsel_b_none_p_kernel(
         gate_rows = held.tile([P, P], F32, name="gate_rows")
         gate_cols = held.tile([P, P], F32, name="gate_cols")
         identity = held.tile([P, P], F32, name="identity")
-
-        def placed(shape, dtype, name, offset):
-            return shared.tile(shape, dtype, name=name, offset=offset, align_bytes=64)
-
-        s1_all = placed([P, COLUMNS], U8, "s1_all", W2_ALL_AT)
-        zeros = placed([P, T], U8, "zeros", ZEROS_AT)
+        s1_all = held.tile([P, COLUMNS], U8, name="s1_all", align_bytes=64)
+        s2_all = held.tile([P, COLUMNS], U8, name="s2_all", align_bytes=64)
         x_plane = held.tile([P, T], U8, name="x_plane", align_bytes=64)
-        nc.vector.memset(s1_all[:].bitcast(I32), 0)
-        nc.vector.memset(zeros[:].bitcast(I32), 0)
-        nc.vector.tensor_copy(out=x_plane[:].bitcast(I32), in_=zeros[:].bitcast(I32))
-        s2_all = placed([P, COLUMNS], U8, "s2_all", S2_ALL_AT)
-        nc.vector.memset(s2_all[:].bitcast(I32), 0)
-        make_identity(nc, identity[:])
+        s2 = held.tile([P, G * WIDTH], U8, name="s2", align_bytes=64)
+        w1_all = held.tile([P, COLUMNS], U32, name="w1_all", align_bytes=64)
+        w2_all = shared.tile([P, COLUMNS], U32, name="w2_all", offset=0, align_bytes=64)
+
+        for plane in (s1_all, s2_all, x_plane, s2):
+            nc.vector.memset(plane[:].bitcast(I32), 0)
+        nc.vector.memset(identity[:], 0.0)
+        make_identity(nc, identity[:], nomemset=True)
 
         nc.sync.dma_start(list1[:], offs)
+        nc.sync.dma_start(list2[:], offs2)
         load_scale_rows(nc, s1_all, w1_scales, W1_ROW)
-        w1_all = placed([P, COLUMNS], U32, "w1_all", W1_ALL_AT)
+        nc.sync.dma_start(out=s2_all[0:P:8, :].bitcast(I32), in_=w2_scales[0].bitcast(I32))
         load_words(nc, w1_all, w1_words)
-        load_words(nc, x_codes, x_words)
         nc.sync.dma_start(
             out=gate_rows[:],
             in_=gate.rearrange("r p (j t) -> (r p j) t", j=HALVES)[0 : GATE_STEP * P : GATE_STEP, :],
         )
-        nc.sync.dma_start(list2[:], offs2)
+        load_words(nc, x_codes, x_words)
         load_scale_rows(nc, x_plane, x_scales, X_ROW)
-        load_scale_rows(nc, s2_all, w2_scales, W2_ROW)
+        load_words(nc, w2_all, w2_words)
 
-        gate_bank = psum.tile([P, P], F32, name="gate_bank", tag="sums", bufs=3)
+        gate_bank = psum.tile([P, P], F32, name="gate_bank", tag="sums", bufs=4)
         nc.tensor.transpose(gate_bank[:], gate_rows[:], identity[:])
         nc.scalar.activation(out=gate_cols[:], in_=gate_bank[:], func=COPY)
 
@@ -92,23 +88,24 @@ def tile_moe_wsel_b_none_p_kernel(
         per_expert = WIDTH // PER_COLUMN
         s1 = held.tile([P, G * WIDTH], U8, name="s1", align_bytes=64)
         nc.vector.tensor_copy(out=s1[:], in_=s1_all[:].indirect(list1[:]))
-        w2_all = placed([P, COLUMNS], U32, "w2_all", W2_ALL_AT)
-        load_words(nc, w2_all, w2_words)
+        s2_spread = held.tile([P, G * WIDTH], U8, name="s2_spread", align_bytes=64)
+        nc.vector.tensor_copy(out=s2_spread[:], in_=s2_all[:].indirect(list2[:]))
+        for v in range(4):
+            nc.sync.dma_start(
+                out=s2[W2_ROW + v : P : 32, :].bitcast(I32), in_=s2_spread[8 * v : P : 32, :].bitcast(I32)
+            )
         w1 = []
         for r in range(G):
             w1.append(held.tile([P, WIDTH], U32, name="w1_%d" % r, align_bytes=64))
             nc.vector.tensor_copy(
                 out=w1[r][:], in_=w1_all[:].indirect(list1[:, r * per_expert : (r + 1) * per_expert])
             )
-        s2 = held.tile([P, G * WIDTH], U8, name="s2", align_bytes=64)
-        nc.vector.tensor_copy(out=s2[:], in_=s2_all[:].indirect(list2[:]))
 
-        h_grouped = []
+        h_grouped = {}
         for r in range(G):
-            turned = psum.tile([P, HALVES, 2, P], F32, name="turned", tag="turned", bufs=2)
             for j in range(HALVES):
                 tokens = slice(j * P, (j + 1) * P)
-                sums = psum.tile([P, WIDTH], F32, name="sums", tag="sums", bufs=3)
+                sums = psum.tile([P, WIDTH], F32, name="sums", tag="sums", bufs=4)
                 nc.tensor.matmul_mx(
                     out=sums[:],
                     lhsT=x_codes[:, tokens].bitcast(FP8X4),
@@ -119,39 +116,46 @@ def tile_moe_wsel_b_none_p_kernel(
                     stop=True,
                 )
                 h_rows = held.tile([P, 2, P, 2], BF16, name="h_rows_%d_%d" % (r, j))
-                nc.scalar.activation(
-                    out=h_rows[:],
-                    in_=sums[:].rearrange("t (p u e) -> t u p e", u=2, e=2),
-                    func=COPY,
-                    scale=gate_column(r, j),
-                )
+                dealt = sums[:].rearrange("t (p u e) -> t u p e", u=2, e=2)
+                if r == VECTOR_EXPERT:
+                    nc.vector.tensor_scalar(
+                        out=h_rows[:], in0=dealt, scalar1=gate_column(r, j), scalar2=None, op0=MULT
+                    )
+                else:
+                    nc.scalar.activation(out=h_rows[:], in_=dealt, func=COPY, scale=gate_column(r, j))
                 pairs = h_rows[:].rearrange("t u p e -> t (u p e)").bitcast(F32)
+                turned = psum.tile([P, 2, P], F32, name="turned", tag="turned", bufs=2)
                 for u in range(2):
-                    nc.tensor.transpose(turned[:, j, u, :], pairs[:, u * P : (u + 1) * P], identity[:])
-            h_grouped.append(held.tile([P, T * 4], BF16, name="h_grouped_%d" % r, align_bytes=64))
-            nc.scalar.copy(
-                out=h_grouped[r][:].bitcast(F32).rearrange("p (j t u) -> p j t u", j=HALVES, u=2),
-                in_=turned[:].rearrange("p j u t -> p j t u"),
+                    nc.tensor.transpose(turned[:, u, :], pairs[:, u * P : (u + 1) * P], identity[:])
+                h_grouped[r, j] = held.tile([P, P * 4], BF16, name="h_grouped_%d_%d" % (r, j), align_bytes=64)
+                nc.scalar.copy(
+                    out=h_grouped[r, j][:].bitcast(F32).rearrange("p (t u) -> p t u", u=2),
+                    in_=turned[:].rearrange("p u t -> p t u"),
+                )
+
+        w2 = []
+        for r in range(G):
+            w2.append(held.tile([P, WIDTH], U32, name="w2_%d" % r, align_bytes=64))
+            nc.vector.tensor_copy(
+                out=w2[r][:], in_=w2_all[:].indirect(list2[:, r * per_expert : (r + 1) * per_expert])
             )
 
         y_sums = [psum.tile([P, WIDTH], F32, name="y_sums_%d" % j) for j in range(HALVES)]
-        keep = []
         for r in range(G):
-            h_codes = placed([P, T], U32, "h_codes_%d" % r, S2_ALL_AT + 4 * T * r)
-            h_plane = held.tile([P, T], U8, name="h_plane", bufs=2, align_bytes=64)
-            nc.vector.quantize_mx(out=h_codes[:].bitcast(FP8X4), scales=h_plane[:], in_=h_grouped[r][:])
-            w2 = held.tile([P, WIDTH], U32, name="w2_%d" % r, align_bytes=64)
-            nc.vector.tensor_copy(
-                out=w2[:], in_=w2_all[:].indirect(list2[:, r * per_expert : (r + 1) * per_expert])
-            )
-            keep.append((h_codes, w2))
             for j in range(HALVES):
-                tokens = slice(j * P, (j + 1) * P)
+                if r == 0:
+                    h_codes = held.tile([P, P], U32, name="h_codes_%d_%d" % (r, j), align_bytes=64)
+                else:
+                    h_codes = shared.tile(
+                        [P, P], U32, name="h_codes_%d_%d" % (r, j), offset=4 * P * (HALVES * r + j), align_bytes=64
+                    )
+                h_plane = held.tile([P, P], U8, name="h_plane_%d_%d" % (r, j), align_bytes=64)
+                nc.vector.quantize_mx(out=h_codes[:].bitcast(FP8X4), scales=h_plane[:], in_=h_grouped[r, j][:])
                 nc.tensor.matmul_mx(
                     out=y_sums[j][:],
-                    lhsT=h_codes[:, tokens].bitcast(FP8X4),
-                    lhsT_scale=h_plane[:, tokens],
-                    rhs=w2[:].bitcast(FP8X4),
+                    lhsT=h_codes[:].bitcast(FP8X4),
+                    lhsT_scale=h_plane[:],
+                    rhs=w2[r][:].bitcast(FP8X4),
                     rhs_scale=s2[W2_ROW:P, r * WIDTH : (r + 1) * WIDTH],
                     start=(r == 0),
                     stop=(r == G - 1),
@@ -167,16 +171,15 @@ def tile_moe_wsel_b_none_p_kernel(
                 nc.scalar.copy(out=y_rows[:], in_=dealt)
             else:
                 nc.vector.tensor_copy(out=y_rows[:], in_=dealt)
-            y_turned = psum.tile([P, 4, P], F32, name="y_turned", tag="sums", bufs=3)
-            for d in range(4):
-                nc.tensor.transpose(y_turned[:, d, :], y_rows[:, d, :], identity[:])
+            for_codes = psum.tile([P, 4, P], F32, name="for_codes", tag="sums", bufs=4)
+            for_out = psum.tile([P, 4, P], F32, name="for_out", tag="sums", bufs=4)
+            for bank in (for_codes, for_out):
+                for d in range(4):
+                    nc.tensor.transpose(bank[:, d, :], y_rows[:, d, :], identity[:])
+            nc.vector.tensor_copy(out=y_grouped[:, tokens, :], in_=for_codes[:].rearrange("p d t -> p t d"))
             y = held.tile([P, 4, P], F32, name="y_%d" % j)
-            if j == 1:
-                nc.vector.tensor_copy(out=y_grouped[:, tokens, :], in_=y_turned[:].rearrange("p d t -> p t d"))
-            nc.scalar.copy(out=y[:], in_=y_turned[:])
+            nc.scalar.copy(out=y[:], in_=for_out[:])
             nc.sync.dma_start(out=out_rows[:, :, tokens], in_=y[:])
-            if j == 0:
-                nc.vector.tensor_copy(out=y_grouped[:, tokens, :], in_=y[:].rearrange("p d t -> p t d"))
 
         y_codes = held.tile([P, T], U32, name="y_codes", align_bytes=64)
         y_plane = held.tile([P, T], U8, name="y_plane", align_bytes=64)

@@ -22,7 +22,8 @@ HALVES = T // P
 PER_COLUMN = 16
 X_ROW, W1_ROW, W2_ROW = 8, 0, 4
 GATE_STEP = 5
-VECTOR_EXPERT = 1
+EARLY = 768
+W1_FIRST_AT = 4 * COLUMNS
 
 FLOPS = 2 * 2 * G * WIDTH * WIDTH * T
 
@@ -88,15 +89,14 @@ def tile_moe_wsel_b_none_p_kernel(
         per_expert = WIDTH // PER_COLUMN
         s1 = held.tile([P, G * WIDTH], U8, name="s1", align_bytes=64)
         nc.vector.tensor_copy(out=s1[:], in_=s1_all[:].indirect(list1[:]))
-        s2_spread = held.tile([P, G * WIDTH], U8, name="s2_spread", align_bytes=64)
-        nc.vector.tensor_copy(out=s2_spread[:], in_=s2_all[:].indirect(list2[:]))
-        for v in range(4):
-            nc.sync.dma_start(
-                out=s2[W2_ROW + v : P : 32, :].bitcast(I32), in_=s2_spread[8 * v : P : 32, :].bitcast(I32)
-            )
+        s2_early = held.tile([P, EARLY], U8, name="s2_early", align_bytes=64)
+        nc.vector.tensor_copy(out=s2_early[:], in_=s2_all[:].indirect(list2[:, : EARLY // PER_COLUMN]))
         w1 = []
         for r in range(G):
-            w1.append(held.tile([P, WIDTH], U32, name="w1_%d" % r, align_bytes=64))
+            if r == 0:
+                w1.append(shared.tile([P, WIDTH], U32, name="w1_0", offset=W1_FIRST_AT, align_bytes=64))
+            else:
+                w1.append(held.tile([P, WIDTH], U32, name="w1_%d" % r, align_bytes=64))
             nc.vector.tensor_copy(
                 out=w1[r][:], in_=w1_all[:].indirect(list1[:, r * per_expert : (r + 1) * per_expert])
             )
@@ -117,12 +117,7 @@ def tile_moe_wsel_b_none_p_kernel(
                 )
                 h_rows = held.tile([P, 2, P, 2], BF16, name="h_rows_%d_%d" % (r, j))
                 dealt = sums[:].rearrange("t (p u e) -> t u p e", u=2, e=2)
-                if r == VECTOR_EXPERT:
-                    nc.vector.tensor_scalar(
-                        out=h_rows[:], in0=dealt, scalar1=gate_column(r, j), scalar2=None, op0=MULT
-                    )
-                else:
-                    nc.scalar.activation(out=h_rows[:], in_=dealt, func=COPY, scale=gate_column(r, j))
+                nc.scalar.activation(out=h_rows[:], in_=dealt, func=COPY, scale=gate_column(r, j))
                 pairs = h_rows[:].rearrange("t u p e -> t (u p e)").bitcast(F32)
                 turned = psum.tile([P, 2, P], F32, name="turned", tag="turned", bufs=2)
                 for u in range(2):
@@ -133,14 +128,33 @@ def tile_moe_wsel_b_none_p_kernel(
                     in_=turned[:].rearrange("p u t -> p t u"),
                 )
 
+        s2_late = shared.tile([P, G * WIDTH - EARLY], U8, name="s2_late", offset=W1_FIRST_AT, align_bytes=64)
+        nc.vector.tensor_copy(out=s2_late[:], in_=s2_all[:].indirect(list2[:, EARLY // PER_COLUMN :]))
+        s2_dealt = held.tile([P, G, 4, P], U8, name="s2_dealt", align_bytes=64)
+        half = P // 2
+        nc.vector.tensor_copy(out=s2_dealt[:, 0], in_=s2_early[:, :WIDTH].rearrange("q (p d) -> q d p", d=4))
+        nc.vector.tensor_copy(
+            out=s2_dealt[:, 1, :, :half], in_=s2_early[:, WIDTH:].rearrange("q (p d) -> q d p", d=4)
+        )
+        nc.vector.tensor_copy(
+            out=s2_dealt[:, 1, :, half:], in_=s2_late[:, : 4 * half].rearrange("q (p d) -> q d p", d=4)
+        )
+        nc.vector.tensor_copy(out=s2_dealt[:, 2], in_=s2_late[:, 4 * half :].rearrange("q (p d) -> q d p", d=4))
+        dealt_rows = s2_dealt[:].rearrange("q r d p -> q (r d p)")
+        for v in range(4):
+            nc.sync.dma_start(
+                out=s2[W2_ROW + v : P : 32, :].bitcast(I32), in_=dealt_rows[8 * v : P : 32, :].bitcast(I32)
+            )
+
         w2 = []
         for r in range(G):
             w2.append(held.tile([P, WIDTH], U32, name="w2_%d" % r, align_bytes=64))
             nc.vector.tensor_copy(
-                out=w2[r][:], in_=w2_all[:].indirect(list2[:, r * per_expert : (r + 1) * per_expert])
+                out=w2[r][:].rearrange("q (d p) -> q p d", d=4),
+                in_=w2_all[:].indirect(list2[:, r * per_expert : (r + 1) * per_expert]),
             )
 
-        y_sums = [psum.tile([P, WIDTH], F32, name="y_sums_%d" % j) for j in range(HALVES)]
+        y_sums = [psum.tile([P, 4, P], F32, name="y_sums_%d" % j) for j in range(HALVES)]
         for r in range(G):
             for j in range(HALVES):
                 if r == 0:
@@ -151,34 +165,25 @@ def tile_moe_wsel_b_none_p_kernel(
                     )
                 h_plane = held.tile([P, P], U8, name="h_plane_%d_%d" % (r, j), align_bytes=64)
                 nc.vector.quantize_mx(out=h_codes[:].bitcast(FP8X4), scales=h_plane[:], in_=h_grouped[r, j][:])
-                nc.tensor.matmul_mx(
-                    out=y_sums[j][:],
-                    lhsT=h_codes[:].bitcast(FP8X4),
-                    lhsT_scale=h_plane[:],
-                    rhs=w2[r][:].bitcast(FP8X4),
-                    rhs_scale=s2[W2_ROW:P, r * WIDTH : (r + 1) * WIDTH],
-                    start=(r == 0),
-                    stop=(r == G - 1),
-                )
+                for d in range(4):
+                    nc.tensor.matmul_mx(
+                        out=y_sums[j][:, d, :],
+                        lhsT=w2[r][:, d * P : (d + 1) * P].bitcast(FP8X4),
+                        lhsT_scale=s2[W2_ROW:P, r * WIDTH + d * P : r * WIDTH + (d + 1) * P],
+                        rhs=h_codes[:].bitcast(FP8X4),
+                        rhs_scale=h_plane[:],
+                        start=(r == 0 and d == 0),
+                        stop=(r == G - 1 and d == 3),
+                    )
 
         y_grouped = held.tile([P, T, 4], BF16, name="y_grouped", align_bytes=64)
         out_rows = out_0.rearrange("(p d) t -> p d t", d=4)
         for j in range(HALVES):
             tokens = slice(j * P, (j + 1) * P)
-            y_rows = held.tile([P, 4, P], F32, name="y_rows_%d" % j)
-            dealt = y_sums[j][:].rearrange("t (p d) -> t d p", d=4)
-            if j == 0:
-                nc.scalar.copy(out=y_rows[:], in_=dealt)
-            else:
-                nc.vector.tensor_copy(out=y_rows[:], in_=dealt)
-            for_codes = psum.tile([P, 4, P], F32, name="for_codes", tag="sums", bufs=4)
-            for_out = psum.tile([P, 4, P], F32, name="for_out", tag="sums", bufs=4)
-            for bank in (for_codes, for_out):
-                for d in range(4):
-                    nc.tensor.transpose(bank[:, d, :], y_rows[:, d, :], identity[:])
-            nc.vector.tensor_copy(out=y_grouped[:, tokens, :], in_=for_codes[:].rearrange("p d t -> p t d"))
+            copy = nc.vector.tensor_copy if j == 0 else nc.scalar.copy
+            copy(out=y_grouped[:, tokens, :], in_=y_sums[j][:].rearrange("p d t -> p t d"))
             y = held.tile([P, 4, P], F32, name="y_%d" % j)
-            nc.scalar.copy(out=y[:], in_=for_out[:])
+            copy(out=y[:], in_=y_sums[j][:])
             nc.sync.dma_start(out=out_rows[:, :, tokens], in_=y[:])
 
         y_codes = held.tile([P, T], U32, name="y_codes", align_bytes=64)

@@ -21,17 +21,17 @@ COLUMNS = 3072
 HALVES = T // P
 PER_COLUMN = 16
 X_ROW, W1_ROW, W2_ROW = 8, 0, 4
-GATE_STEP = 5
-EARLY = 768
-W1_FIRST_AT = 4 * COLUMNS
+GATE_AT = 4 * COLUMNS
+ON_VECTOR = (1, 1)
+WARM_PASSES = 12
 
 FLOPS = 2 * 2 * G * WIDTH * WIDTH * T
 
 
-def load_scale_rows(nc, plane, scales, first_row):
+def load_scale_rows(queues, plane, scales, first_row):
     rows = scales[0].bitcast(I32)
     for v in range(4):
-        nc.sync.dma_start(out=plane[first_row + v : P : 32, :].bitcast(I32), in_=rows[v:16:4, :])
+        queues[v].dma_start(out=plane[first_row + v : P : 32, :].bitcast(I32), in_=rows[v:16:4, :])
 
 
 def load_words(nc, tile, words):
@@ -50,8 +50,8 @@ def tile_moe_wsel_b_none_p_kernel(
         list1 = held.tile([P, G * WIDTH // PER_COLUMN], U16, name="list1")
         list2 = held.tile([P, G * WIDTH // PER_COLUMN], U16, name="list2")
         x_codes = held.tile([P, T], U32, name="x_codes", align_bytes=64)
-        gate_rows = held.tile([P, P], F32, name="gate_rows")
-        gate_cols = held.tile([P, P], F32, name="gate_cols")
+        gate_rows = shared.tile([P, T], F32, name="gate_rows", offset=GATE_AT, align_bytes=64)
+        gate_cols = held.tile([P, HALVES, G], F32, name="gate_cols")
         identity = held.tile([P, P], F32, name="identity")
         s1_all = held.tile([P, COLUMNS], U8, name="s1_all", align_bytes=64)
         s2_all = held.tile([P, COLUMNS], U8, name="s2_all", align_bytes=64)
@@ -60,43 +60,66 @@ def tile_moe_wsel_b_none_p_kernel(
         w1_all = held.tile([P, COLUMNS], U32, name="w1_all", align_bytes=64)
         w2_all = shared.tile([P, COLUMNS], U32, name="w2_all", offset=0, align_bytes=64)
 
-        for plane in (s1_all, s2_all, x_plane, s2):
+        for plane in (s2_all, s1_all, x_plane, s2):
             nc.vector.memset(plane[:].bitcast(I32), 0)
+        nc.vector.memset(gate_rows[:], 0.0)
         nc.vector.memset(identity[:], 0.0)
         make_identity(nc, identity[:], nomemset=True)
+        zeros = held.tile([P, 4 * P], BF16, name="zeros", align_bytes=64)
+        nc.vector.memset(zeros[:].bitcast(I32), 0)
+        warm_codes = held.tile([P, P], U32, name="warm_codes", align_bytes=64)
+        warm_plane = held.tile([P, P], U8, name="warm_plane", align_bytes=64)
+        nc.vector.quantize_mx(out=warm_codes[:].bitcast(FP8X4), scales=warm_plane[:], in_=zeros[:])
 
-        nc.sync.dma_start(list1[:], offs)
         nc.sync.dma_start(list2[:], offs2)
-        load_scale_rows(nc, s1_all, w1_scales, W1_ROW)
+        nc.sync.dma_start(list1[:], offs)
         nc.sync.dma_start(out=s2_all[0:P:8, :].bitcast(I32), in_=w2_scales[0].bitcast(I32))
+        load_scale_rows([nc.scalar, nc.scalar, nc.sync, nc.sync], s1_all, w1_scales, W1_ROW)
         load_words(nc, w1_all, w1_words)
-        nc.sync.dma_start(
-            out=gate_rows[:],
-            in_=gate.rearrange("r p (j t) -> (r p j) t", j=HALVES)[0 : GATE_STEP * P : GATE_STEP, :],
-        )
+        nc.sync.dma_start(out=gate_rows[:G, :], in_=gate[:, 0, :])
         load_words(nc, x_codes, x_words)
-        load_scale_rows(nc, x_plane, x_scales, X_ROW)
+        load_scale_rows([nc.sync] * 4, x_plane, x_scales, X_ROW)
         load_words(nc, w2_all, w2_words)
 
-        gate_bank = psum.tile([P, P], F32, name="gate_bank", tag="sums", bufs=4)
-        nc.tensor.transpose(gate_bank[:], gate_rows[:], identity[:])
-        nc.scalar.activation(out=gate_cols[:], in_=gate_bank[:], func=COPY)
+        gate_bank = psum.tile([P, HALVES, P], F32, name="gate_bank", tag="sums", bufs=3)
+        for j in range(HALVES):
+            nc.tensor.transpose(gate_bank[:, j, :], gate_rows[:, j * P : (j + 1) * P], identity[:])
+        nc.scalar.activation(out=gate_cols[:], in_=gate_bank[:, :, :G], func=COPY)
 
         def gate_column(r, j):
-            a = 2 * -(-r * P * HALVES // (2 * GATE_STEP)) + j
-            return gate_cols[:, a : a + 1]
+            return gate_cols[:, j, r : r + 1]
 
         per_expert = WIDTH // PER_COLUMN
-        s1 = held.tile([P, G * WIDTH], U8, name="s1", align_bytes=64)
-        nc.vector.tensor_copy(out=s1[:], in_=s1_all[:].indirect(list1[:]))
-        s2_early = held.tile([P, EARLY], U8, name="s2_early", align_bytes=64)
-        nc.vector.tensor_copy(out=s2_early[:], in_=s2_all[:].indirect(list2[:, : EARLY // PER_COLUMN]))
+        s2_spread = held.tile([P, G * WIDTH], U8, name="s2_spread", align_bytes=64)
+        nc.vector.tensor_copy(out=s2_spread[:], in_=s2_all[:].indirect(list2[:]))
+        warm = psum.tile([P, P], F32, name="warm", tag="turned", bufs=3)
+        for a in range(WARM_PASSES):
+            nc.tensor.matmul_mx(
+                out=warm[:],
+                lhsT=warm_codes[:].bitcast(FP8X4),
+                lhsT_scale=warm_plane[:],
+                rhs=warm_codes[:].bitcast(FP8X4),
+                rhs_scale=s2_spread[:, :P],
+                start=True,
+                stop=True,
+            )
+        s2_dealt = held.tile([P, G * WIDTH], U8, name="s2_dealt", align_bytes=64)
+        nc.vector.tensor_copy(
+            out=s2_dealt[:].rearrange("q (r d p) -> q d r p", r=G, d=4),
+            in_=s2_spread[:].rearrange("q (r p d) -> q d r p", r=G, d=4),
+        )
+        for v in range(4):
+            nc.sync.dma_start(
+                out=s2[W2_ROW + v : P : 32, :].bitcast(I32), in_=s2_dealt[8 * v : P : 32, :].bitcast(I32)
+            )
+        s1_early = held.tile([P, (G - 1) * WIDTH], U8, name="s1_early", align_bytes=64)
+        nc.vector.tensor_copy(out=s1_early[:], in_=s1_all[:].indirect(list1[:, : (G - 1) * per_expert]))
+        s1_late = shared.tile([P, WIDTH], U8, name="s1_late", offset=GATE_AT, align_bytes=64)
+        nc.vector.tensor_copy(out=s1_late[:], in_=s1_all[:].indirect(list1[:, (G - 1) * per_expert :]))
+        s1 = [s1_early[W1_ROW:P, r * WIDTH : (r + 1) * WIDTH] for r in range(G - 1)] + [s1_late[W1_ROW:P, :]]
         w1 = []
         for r in range(G):
-            if r == 0:
-                w1.append(shared.tile([P, WIDTH], U32, name="w1_0", offset=W1_FIRST_AT, align_bytes=64))
-            else:
-                w1.append(held.tile([P, WIDTH], U32, name="w1_%d" % r, align_bytes=64))
+            w1.append(held.tile([P, WIDTH], U32, name="w1_%d" % r, align_bytes=64))
             nc.vector.tensor_copy(
                 out=w1[r][:], in_=w1_all[:].indirect(list1[:, r * per_expert : (r + 1) * per_expert])
             )
@@ -105,21 +128,26 @@ def tile_moe_wsel_b_none_p_kernel(
         for r in range(G):
             for j in range(HALVES):
                 tokens = slice(j * P, (j + 1) * P)
-                sums = psum.tile([P, WIDTH], F32, name="sums", tag="sums", bufs=4)
+                sums = psum.tile([P, WIDTH], F32, name="sums", tag="sums", bufs=3)
                 nc.tensor.matmul_mx(
                     out=sums[:],
                     lhsT=x_codes[:, tokens].bitcast(FP8X4),
                     lhsT_scale=x_plane[X_ROW:P, tokens],
                     rhs=w1[r][:].bitcast(FP8X4),
-                    rhs_scale=s1[W1_ROW:P, r * WIDTH : (r + 1) * WIDTH],
+                    rhs_scale=s1[r],
                     start=True,
                     stop=True,
                 )
                 h_rows = held.tile([P, 2, P, 2], BF16, name="h_rows_%d_%d" % (r, j))
                 dealt = sums[:].rearrange("t (p u e) -> t u p e", u=2, e=2)
-                nc.scalar.activation(out=h_rows[:], in_=dealt, func=COPY, scale=gate_column(r, j))
+                if (r, j) == ON_VECTOR:
+                    nc.vector.tensor_scalar(
+                        out=h_rows[:], in0=dealt, scalar1=gate_column(r, j), scalar2=None, op0=MULT
+                    )
+                else:
+                    nc.scalar.activation(out=h_rows[:], in_=dealt, func=COPY, scale=gate_column(r, j))
                 pairs = h_rows[:].rearrange("t u p e -> t (u p e)").bitcast(F32)
-                turned = psum.tile([P, 2, P], F32, name="turned", tag="turned", bufs=2)
+                turned = psum.tile([P, 2, P], F32, name="turned", tag="turned", bufs=3)
                 for u in range(2):
                     nc.tensor.transpose(turned[:, u, :], pairs[:, u * P : (u + 1) * P], identity[:])
                 h_grouped[r, j] = held.tile([P, P * 4], BF16, name="h_grouped_%d_%d" % (r, j), align_bytes=64)
@@ -127,24 +155,6 @@ def tile_moe_wsel_b_none_p_kernel(
                     out=h_grouped[r, j][:].bitcast(F32).rearrange("p (t u) -> p t u", u=2),
                     in_=turned[:].rearrange("p u t -> p t u"),
                 )
-
-        s2_late = shared.tile([P, G * WIDTH - EARLY], U8, name="s2_late", offset=W1_FIRST_AT, align_bytes=64)
-        nc.vector.tensor_copy(out=s2_late[:], in_=s2_all[:].indirect(list2[:, EARLY // PER_COLUMN :]))
-        s2_dealt = held.tile([P, G, 4, P], U8, name="s2_dealt", align_bytes=64)
-        half = P // 2
-        nc.vector.tensor_copy(out=s2_dealt[:, 0], in_=s2_early[:, :WIDTH].rearrange("q (p d) -> q d p", d=4))
-        nc.vector.tensor_copy(
-            out=s2_dealt[:, 1, :, :half], in_=s2_early[:, WIDTH:].rearrange("q (p d) -> q d p", d=4)
-        )
-        nc.vector.tensor_copy(
-            out=s2_dealt[:, 1, :, half:], in_=s2_late[:, : 4 * half].rearrange("q (p d) -> q d p", d=4)
-        )
-        nc.vector.tensor_copy(out=s2_dealt[:, 2], in_=s2_late[:, 4 * half :].rearrange("q (p d) -> q d p", d=4))
-        dealt_rows = s2_dealt[:].rearrange("q r d p -> q (r d p)")
-        for v in range(4):
-            nc.sync.dma_start(
-                out=s2[W2_ROW + v : P : 32, :].bitcast(I32), in_=dealt_rows[8 * v : P : 32, :].bitcast(I32)
-            )
 
         w2 = []
         for r in range(G):
@@ -180,17 +190,25 @@ def tile_moe_wsel_b_none_p_kernel(
         out_rows = out_0.rearrange("(p d) t -> p d t", d=4)
         for j in range(HALVES):
             tokens = slice(j * P, (j + 1) * P)
-            copy = nc.vector.tensor_copy if j == 0 else nc.scalar.copy
-            copy(out=y_grouped[:, tokens, :], in_=y_sums[j][:].rearrange("p d t -> p t d"))
             y = held.tile([P, 4, P], F32, name="y_%d" % j)
-            copy(out=y[:], in_=y_sums[j][:])
+            regrouped = y_sums[j][:].rearrange("p d t -> p t d")
+            if j == 0:
+                nc.vector.tensor_copy(out=y[:], in_=y_sums[j][:])
+                nc.vector.tensor_copy(out=y_grouped[:, tokens, :], in_=regrouped)
+            else:
+                nc.scalar.copy(out=y_grouped[:, tokens, :], in_=regrouped)
+                nc.scalar.copy(out=y[:], in_=y_sums[j][:])
             nc.sync.dma_start(out=out_rows[:, :, tokens], in_=y[:])
 
         y_codes = held.tile([P, T], U32, name="y_codes", align_bytes=64)
         y_plane = held.tile([P, T], U8, name="y_plane", align_bytes=64)
-        nc.vector.quantize_mx(
-            out=y_codes[:].bitcast(FP8X4), scales=y_plane[:], in_=y_grouped[:].rearrange("p t d -> p (t d)")
-        )
+        for j in reversed(range(HALVES)):
+            tokens = slice(j * P, (j + 1) * P)
+            nc.vector.quantize_mx(
+                out=y_codes[:, tokens].bitcast(FP8X4),
+                scales=y_plane[:, tokens],
+                in_=y_grouped[:, tokens, :].rearrange("p t d -> p (t d)"),
+            )
         nc.sync.dma_start(
             out=out_1[0].rearrange("p t d -> p (t d)").bitcast(I32), in_=y_codes[:].bitcast(I32)
         )

@@ -74,7 +74,7 @@ def tile_moe_wsel_b_none_p_kernel(
         nc.sync.dma_start(list2[:], offs2)
         nc.sync.dma_start(list1[:], offs)
         nc.sync.dma_start(out=s2_all[0:P:8, :].bitcast(I32), in_=w2_scales[0].bitcast(I32))
-        load_scale_rows([nc.scalar, nc.scalar, nc.sync, nc.sync], s1_all, w1_scales, W1_ROW)
+        load_scale_rows([nc.sync] * 4, s1_all, w1_scales, W1_ROW)
         load_words(nc, w1_all, w1_words)
         nc.sync.dma_start(out=gate_rows[:G, :], in_=gate[:, 0, :])
         load_words(nc, x_codes, x_words)

@@ -23,7 +23,6 @@ PER_COLUMN = 16
 X_ROW, W1_ROW, W2_ROW = 8, 0, 4
 GATE_AT = 4 * COLUMNS
 ON_VECTOR = (1, 1)
-WARM_PASSES = 12
 
 FLOPS = 2 * 2 * G * WIDTH * WIDTH * T
 
@@ -65,11 +64,6 @@ def tile_moe_wsel_b_none_p_kernel(
         nc.vector.memset(gate_rows[:], 0.0)
         nc.vector.memset(identity[:], 0.0)
         make_identity(nc, identity[:], nomemset=True)
-        zeros = held.tile([P, 4 * P], BF16, name="zeros", align_bytes=64)
-        nc.vector.memset(zeros[:].bitcast(I32), 0)
-        warm_codes = held.tile([P, P], U32, name="warm_codes", align_bytes=64)
-        warm_plane = held.tile([P, P], U8, name="warm_plane", align_bytes=64)
-        nc.vector.quantize_mx(out=warm_codes[:].bitcast(FP8X4), scales=warm_plane[:], in_=zeros[:])
 
         nc.sync.dma_start(list2[:], offs2)
         nc.sync.dma_start(list1[:], offs)
@@ -92,17 +86,6 @@ def tile_moe_wsel_b_none_p_kernel(
         per_expert = WIDTH // PER_COLUMN
         s2_spread = held.tile([P, G * WIDTH], U8, name="s2_spread", align_bytes=64)
         nc.vector.tensor_copy(out=s2_spread[:], in_=s2_all[:].indirect(list2[:]))
-        warm = psum.tile([P, P], F32, name="warm", tag="turned", bufs=3)
-        for a in range(WARM_PASSES):
-            nc.tensor.matmul_mx(
-                out=warm[:],
-                lhsT=warm_codes[:].bitcast(FP8X4),
-                lhsT_scale=warm_plane[:],
-                rhs=warm_codes[:].bitcast(FP8X4),
-                rhs_scale=s2_spread[:, :P],
-                start=True,
-                stop=True,
-            )
         s2_dealt = held.tile([P, G * WIDTH], U8, name="s2_dealt", align_bytes=64)
         nc.vector.tensor_copy(
             out=s2_dealt[:].rearrange("q (r d p) -> q d r p", r=G, d=4),

@@ -22,6 +22,7 @@ HALVES = T // P
 PER_COLUMN = 16
 X_ROW, W1_ROW, W2_ROW = 8, 0, 4
 GATE_AT = 4 * COLUMNS
+W1_ALL_AT = GATE_AT + 4 * T
 ON_VECTOR = (1, 1)
 
 FLOPS = 2 * 2 * G * WIDTH * WIDTH * T
@@ -56,19 +57,19 @@ def tile_moe_wsel_b_none_p_kernel(
         s2_all = held.tile([P, COLUMNS], U8, name="s2_all", align_bytes=64)
         x_plane = held.tile([P, T], U8, name="x_plane", align_bytes=64)
         s2 = held.tile([P, G * WIDTH], U8, name="s2", align_bytes=64)
-        w1_all = held.tile([P, COLUMNS], U32, name="w1_all", align_bytes=64)
+        w1_all = shared.tile([P, COLUMNS], U32, name="w1_all", offset=W1_ALL_AT, align_bytes=64)
         w2_all = shared.tile([P, COLUMNS], U32, name="w2_all", offset=0, align_bytes=64)
 
-        for plane in (s2_all, s1_all, x_plane, s2):
+        for plane in (s1_all, s2_all, x_plane, s2):
             nc.vector.memset(plane[:].bitcast(I32), 0)
         nc.vector.memset(gate_rows[:], 0.0)
         nc.vector.memset(identity[:], 0.0)
         make_identity(nc, identity[:], nomemset=True)
 
-        nc.sync.dma_start(list2[:], offs2)
         nc.sync.dma_start(list1[:], offs)
-        nc.sync.dma_start(out=s2_all[0:P:8, :].bitcast(I32), in_=w2_scales[0].bitcast(I32))
+        nc.sync.dma_start(list2[:], offs2)
         load_scale_rows([nc.sync] * 4, s1_all, w1_scales, W1_ROW)
+        nc.sync.dma_start(out=s2_all[0:P:8, :].bitcast(I32), in_=w2_scales[0].bitcast(I32))
         load_words(nc, w1_all, w1_words)
         nc.sync.dma_start(out=gate_rows[:G, :], in_=gate[:, 0, :])
         load_words(nc, x_codes, x_words)
@@ -84,19 +85,10 @@ def tile_moe_wsel_b_none_p_kernel(
             return gate_cols[:, j, r : r + 1]
 
         per_expert = WIDTH // PER_COLUMN
-        s2_spread = held.tile([P, G * WIDTH], U8, name="s2_spread", align_bytes=64)
-        nc.vector.tensor_copy(out=s2_spread[:], in_=s2_all[:].indirect(list2[:]))
-        s2_dealt = held.tile([P, G * WIDTH], U8, name="s2_dealt", align_bytes=64)
-        nc.vector.tensor_copy(
-            out=s2_dealt[:].rearrange("q (r d p) -> q d r p", r=G, d=4),
-            in_=s2_spread[:].rearrange("q (r p d) -> q d r p", r=G, d=4),
-        )
-        for v in range(4):
-            nc.sync.dma_start(
-                out=s2[W2_ROW + v : P : 32, :].bitcast(I32), in_=s2_dealt[8 * v : P : 32, :].bitcast(I32)
-            )
         s1_early = held.tile([P, (G - 1) * WIDTH], U8, name="s1_early", align_bytes=64)
         nc.vector.tensor_copy(out=s1_early[:], in_=s1_all[:].indirect(list1[:, : (G - 1) * per_expert]))
+        s2_spread = held.tile([P, G * WIDTH], U8, name="s2_spread", align_bytes=64)
+        nc.vector.tensor_copy(out=s2_spread[:], in_=s2_all[:].indirect(list2[:]))
         s1_late = shared.tile([P, WIDTH], U8, name="s1_late", offset=GATE_AT, align_bytes=64)
         nc.vector.tensor_copy(out=s1_late[:], in_=s1_all[:].indirect(list1[:, (G - 1) * per_expert :]))
         s1 = [s1_early[W1_ROW:P, r * WIDTH : (r + 1) * WIDTH] for r in range(G - 1)] + [s1_late[W1_ROW:P, :]]
@@ -105,6 +97,16 @@ def tile_moe_wsel_b_none_p_kernel(
             w1.append(held.tile([P, WIDTH], U32, name="w1_%d" % r, align_bytes=64))
             nc.vector.tensor_copy(
                 out=w1[r][:], in_=w1_all[:].indirect(list1[:, r * per_expert : (r + 1) * per_expert])
+            )
+
+        s2_dealt = shared.tile([P, G * WIDTH], U8, name="s2_dealt", offset=W1_ALL_AT, align_bytes=64)
+        nc.vector.tensor_copy(
+            out=s2_dealt[:].rearrange("q (r d p) -> q d r p", r=G, d=4),
+            in_=s2_spread[:].rearrange("q (r p d) -> q d r p", r=G, d=4),
+        )
+        for v in range(4):
+            nc.sync.dma_start(
+                out=s2[W2_ROW + v : P : 32, :].bitcast(I32), in_=s2_dealt[8 * v : P : 32, :].bitcast(I32)
             )
 
         h_grouped = {}

@@ -21,21 +21,31 @@ COLUMNS = 3072
 HALVES = T // P
 PER_COLUMN = 16
 X_ROW, W1_ROW, W2_ROW = 8, 0, 4
-GATE_AT = 4 * COLUMNS
-W1_ALL_AT = GATE_AT + 4 * T
+W1_FIRST = 1024
+S2_ROW = P - 16
+W1_ALL_AT = 4 * COLUMNS
 ON_VECTOR = (1, 1)
 
 FLOPS = 2 * 2 * G * WIDTH * WIDTH * T
 
 
-def load_scale_rows(queues, plane, scales, first_row):
+def gather(nc, out, window, offsets, first, count):
+    nc.vector.tensor_copy(
+        out=out, in_=window[:].indirect(offsets[:, first // PER_COLUMN : (first + count) // PER_COLUMN])
+    )
+
+
+def load_scale_rows(nc, plane, scales, first_row):
     rows = scales[0].bitcast(I32)
     for v in range(4):
-        queues[v].dma_start(out=plane[first_row + v : P : 32, :].bitcast(I32), in_=rows[v:16:4, :])
+        nc.sync.dma_start(out=plane[first_row + v : P : 32, :].bitcast(I32), in_=rows[v:16:4, :])
 
 
-def load_words(nc, tile, words):
-    nc.sync.dma_start(out=tile[:].bitcast(I32), in_=words[0].rearrange("p m d -> p (m d)").bitcast(I32))
+def load_words(nc, tile, words, first, last):
+    nc.sync.dma_start(
+        out=tile[:, first:last].bitcast(I32),
+        in_=words[0].rearrange("p m d -> p (m d)").bitcast(I32)[:, first:last],
+    )
 
 
 def tile_moe_wsel_b_none_p_kernel(
@@ -50,7 +60,7 @@ def tile_moe_wsel_b_none_p_kernel(
         list1 = held.tile([P, G * WIDTH // PER_COLUMN], U16, name="list1")
         list2 = held.tile([P, G * WIDTH // PER_COLUMN], U16, name="list2")
         x_codes = held.tile([P, T], U32, name="x_codes", align_bytes=64)
-        gate_rows = shared.tile([P, T], F32, name="gate_rows", offset=GATE_AT, align_bytes=64)
+        gate_rows = held.tile([P, T], F32, name="gate_rows")
         gate_cols = held.tile([P, HALVES, G], F32, name="gate_cols")
         identity = held.tile([P, P], F32, name="identity")
         s1_all = held.tile([P, COLUMNS], U8, name="s1_all", align_bytes=64)
@@ -60,54 +70,49 @@ def tile_moe_wsel_b_none_p_kernel(
         w1_all = shared.tile([P, COLUMNS], U32, name="w1_all", offset=W1_ALL_AT, align_bytes=64)
         w2_all = shared.tile([P, COLUMNS], U32, name="w2_all", offset=0, align_bytes=64)
 
-        for plane in (s1_all, s2_all, x_plane, s2):
+        nc.vector.memset(s2_all[:S2_ROW, :].bitcast(I32), 0)
+        for plane in (s1_all, x_plane):
             nc.vector.memset(plane[:].bitcast(I32), 0)
         nc.vector.memset(gate_rows[:], 0.0)
-        nc.vector.memset(identity[:], 0.0)
-        make_identity(nc, identity[:], nomemset=True)
+        make_identity(nc, identity[:])
+        nc.gpsimd.memset(s2[:].bitcast(I32), 0)
 
-        nc.sync.dma_start(list1[:], offs)
+        nc.sync.dma_start(out=s2_all[S2_ROW:, :].bitcast(I32), in_=w2_scales[0].bitcast(I32))
         nc.sync.dma_start(list2[:], offs2)
-        load_scale_rows([nc.sync] * 4, s1_all, w1_scales, W1_ROW)
-        nc.sync.dma_start(out=s2_all[0:P:8, :].bitcast(I32), in_=w2_scales[0].bitcast(I32))
-        load_words(nc, w1_all, w1_words)
+        load_words(nc, w1_all, w1_words, 0, W1_FIRST)
+        nc.sync.dma_start(list1[:], offs)
+        load_scale_rows(nc, s1_all, w1_scales, W1_ROW)
+        load_words(nc, w1_all, w1_words, W1_FIRST, COLUMNS)
         nc.sync.dma_start(out=gate_rows[:G, :], in_=gate[:, 0, :])
-        load_words(nc, x_codes, x_words)
-        load_scale_rows([nc.sync] * 4, x_plane, x_scales, X_ROW)
-        load_words(nc, w2_all, w2_words)
+        load_words(nc, x_codes, x_words, 0, T)
+        load_scale_rows(nc, x_plane, x_scales, X_ROW)
+        load_words(nc, w2_all, w2_words, 0, COLUMNS)
 
         gate_bank = psum.tile([P, HALVES, P], F32, name="gate_bank", tag="sums", bufs=3)
         for j in range(HALVES):
             nc.tensor.transpose(gate_bank[:, j, :], gate_rows[:, j * P : (j + 1) * P], identity[:])
         nc.scalar.activation(out=gate_cols[:], in_=gate_bank[:, :, :G], func=COPY)
 
-        def gate_column(r, j):
-            return gate_cols[:, j, r : r + 1]
-
-        per_expert = WIDTH // PER_COLUMN
-        s1_early = held.tile([P, (G - 1) * WIDTH], U8, name="s1_early", align_bytes=64)
-        nc.vector.tensor_copy(out=s1_early[:], in_=s1_all[:].indirect(list1[:, : (G - 1) * per_expert]))
         s2_spread = held.tile([P, G * WIDTH], U8, name="s2_spread", align_bytes=64)
-        nc.vector.tensor_copy(out=s2_spread[:], in_=s2_all[:].indirect(list2[:]))
-        s1_late = shared.tile([P, WIDTH], U8, name="s1_late", offset=GATE_AT, align_bytes=64)
-        nc.vector.tensor_copy(out=s1_late[:], in_=s1_all[:].indirect(list1[:, (G - 1) * per_expert :]))
-        s1 = [s1_early[W1_ROW:P, r * WIDTH : (r + 1) * WIDTH] for r in range(G - 1)] + [s1_late[W1_ROW:P, :]]
-        w1 = []
-        for r in range(G):
-            w1.append(held.tile([P, WIDTH], U32, name="w1_%d" % r, align_bytes=64))
-            nc.vector.tensor_copy(
-                out=w1[r][:], in_=w1_all[:].indirect(list1[:, r * per_expert : (r + 1) * per_expert])
-            )
-
-        s2_dealt = shared.tile([P, G * WIDTH], U8, name="s2_dealt", offset=W1_ALL_AT, align_bytes=64)
+        gather(nc, s2_spread[:], s2_all, list2, 0, G * WIDTH)
+        s2_dealt = held.tile([P, G * WIDTH], U8, name="s2_dealt", align_bytes=64)
         nc.vector.tensor_copy(
             out=s2_dealt[:].rearrange("q (r d p) -> q d r p", r=G, d=4),
             in_=s2_spread[:].rearrange("q (r p d) -> q d r p", r=G, d=4),
         )
         for v in range(4):
             nc.sync.dma_start(
-                out=s2[W2_ROW + v : P : 32, :].bitcast(I32), in_=s2_dealt[8 * v : P : 32, :].bitcast(I32)
+                out=s2[W2_ROW + v : P : 32, :].bitcast(I32), in_=s2_dealt[S2_ROW + v : P : 4, :].bitcast(I32)
             )
+        s1_early = held.tile([P, (G - 1) * WIDTH], U8, name="s1_early", align_bytes=64)
+        gather(nc, s1_early[:], s1_all, list1, 0, (G - 1) * WIDTH)
+        w1 = []
+        for r in range(G):
+            w1.append(held.tile([P, WIDTH], U32, name="w1_%d" % r, align_bytes=64))
+            gather(nc, w1[r][:], w1_all, list1, r * WIDTH, WIDTH)
+        s1_late = shared.tile([P, WIDTH], U8, name="s1_late", offset=W1_ALL_AT, align_bytes=64)
+        gather(nc, s1_late[:], s1_all, list1, (G - 1) * WIDTH, WIDTH)
+        s1 = [s1_early[:, r * WIDTH : (r + 1) * WIDTH] for r in range(G - 1)] + [s1_late[:]]
 
         h_grouped = {}
         for r in range(G):
@@ -125,12 +130,11 @@ def tile_moe_wsel_b_none_p_kernel(
                 )
                 h_rows = held.tile([P, 2, P, 2], BF16, name="h_rows_%d_%d" % (r, j))
                 dealt = sums[:].rearrange("t (p u e) -> t u p e", u=2, e=2)
+                gate_column = gate_cols[:, j, r : r + 1]
                 if (r, j) == ON_VECTOR:
-                    nc.vector.tensor_scalar(
-                        out=h_rows[:], in0=dealt, scalar1=gate_column(r, j), scalar2=None, op0=MULT
-                    )
+                    nc.vector.tensor_scalar(out=h_rows[:], in0=dealt, scalar1=gate_column, scalar2=None, op0=MULT)
                 else:
-                    nc.scalar.activation(out=h_rows[:], in_=dealt, func=COPY, scale=gate_column(r, j))
+                    nc.scalar.activation(out=h_rows[:], in_=dealt, func=COPY, scale=gate_column)
                 pairs = h_rows[:].rearrange("t u p e -> t (u p e)").bitcast(F32)
                 turned = psum.tile([P, 2, P], F32, name="turned", tag="turned", bufs=3)
                 for u in range(2):
@@ -144,10 +148,7 @@ def tile_moe_wsel_b_none_p_kernel(
         w2 = []
         for r in range(G):
             w2.append(held.tile([P, WIDTH], U32, name="w2_%d" % r, align_bytes=64))
-            nc.vector.tensor_copy(
-                out=w2[r][:].rearrange("q (d p) -> q p d", d=4),
-                in_=w2_all[:].indirect(list2[:, r * per_expert : (r + 1) * per_expert]),
-            )
+            gather(nc, w2[r][:].rearrange("q (d p) -> q p d", d=4), w2_all, list2, r * WIDTH, WIDTH)
 
         y_sums = [psum.tile([P, 4, P], F32, name="y_sums_%d" % j) for j in range(HALVES)]
         for r in range(G):

@@ -21,9 +21,12 @@ COLUMNS = 3072
 HALVES = T // P
 PER_COLUMN = 16
 X_ROW, W1_ROW, W2_ROW = 8, 0, 4
-W1_FIRST = 1024
 S2_ROW = P - 16
 W1_ALL_AT = 4 * COLUMNS
+DEALT_AT = 8 * COLUMNS + 8 * P
+LAST_W2_AT = DEALT_AT + 5 * WIDTH
+LATE_H_AT = {(1, 0): DEALT_AT - 7 * P, (1, 1): DEALT_AT + 3 * P, (2, 0): DEALT_AT + 11 * P}
+WARM_UPS = 3
 ON_VECTOR = (1, 1)
 
 FLOPS = 2 * 2 * G * WIDTH * WIDTH * T
@@ -60,49 +63,60 @@ def tile_moe_wsel_b_none_p_kernel(
         list1 = held.tile([P, G * WIDTH // PER_COLUMN], U16, name="list1")
         list2 = held.tile([P, G * WIDTH // PER_COLUMN], U16, name="list2")
         x_codes = held.tile([P, T], U32, name="x_codes", align_bytes=64)
-        gate_rows = held.tile([P, T], F32, name="gate_rows")
-        gate_cols = held.tile([P, HALVES, G], F32, name="gate_cols")
+        gate_rows = held.tile([P, P], F32, name="gate_rows")
+        gate_cols = held.tile([P, G * HALVES], F32, name="gate_cols")
         identity = held.tile([P, P], F32, name="identity")
         s1_all = held.tile([P, COLUMNS], U8, name="s1_all", align_bytes=64)
         s2_all = held.tile([P, COLUMNS], U8, name="s2_all", align_bytes=64)
         x_plane = held.tile([P, T], U8, name="x_plane", align_bytes=64)
-        s2 = held.tile([P, G * WIDTH], U8, name="s2", align_bytes=64)
+        s2 = held.tile([P, 4 * WIDTH], U8, name="s2", align_bytes=64)
         w1_all = shared.tile([P, COLUMNS], U32, name="w1_all", offset=W1_ALL_AT, align_bytes=64)
         w2_all = shared.tile([P, COLUMNS], U32, name="w2_all", offset=0, align_bytes=64)
 
+        nc.vector.memset(s1_all[:].bitcast(I32), 0)
         nc.vector.memset(s2_all[:S2_ROW, :].bitcast(I32), 0)
-        for plane in (s1_all, x_plane):
-            nc.vector.memset(plane[:].bitcast(I32), 0)
+        nc.vector.memset(x_plane[:].bitcast(I32), 0)
         nc.vector.memset(gate_rows[:], 0.0)
         make_identity(nc, identity[:])
         nc.gpsimd.memset(s2[:].bitcast(I32), 0)
 
         nc.sync.dma_start(out=s2_all[S2_ROW:, :].bitcast(I32), in_=w2_scales[0].bitcast(I32))
         nc.sync.dma_start(list2[:], offs2)
-        load_words(nc, w1_all, w1_words, 0, W1_FIRST)
         nc.sync.dma_start(list1[:], offs)
         load_scale_rows(nc, s1_all, w1_scales, W1_ROW)
-        load_words(nc, w1_all, w1_words, W1_FIRST, COLUMNS)
-        nc.sync.dma_start(out=gate_rows[:G, :], in_=gate[:, 0, :])
+        load_words(nc, w1_all, w1_words, 0, COLUMNS)
+        gate_halves = gate.rearrange("r p (j c) -> (r p j) c", c=P)
+        nc.sync.dma_start(out=gate_rows[: G * HALVES, :], in_=gate_halves[0 : G * HALVES * (P + 1) - P : P + 1, :])
         load_words(nc, x_codes, x_words, 0, T)
         load_scale_rows(nc, x_plane, x_scales, X_ROW)
         load_words(nc, w2_all, w2_words, 0, COLUMNS)
 
-        gate_bank = psum.tile([P, HALVES, P], F32, name="gate_bank", tag="sums", bufs=3)
-        for j in range(HALVES):
-            nc.tensor.transpose(gate_bank[:, j, :], gate_rows[:, j * P : (j + 1) * P], identity[:])
-        nc.scalar.activation(out=gate_cols[:], in_=gate_bank[:, :, :G], func=COPY)
+        gate_bank = psum.tile([P, P], F32, name="gate_bank", tag="turned", bufs=3)
+        nc.tensor.transpose(gate_bank[:], gate_rows[:], identity[:])
+        nc.scalar.activation(out=gate_cols[:], in_=gate_bank[:, : G * HALVES], func=COPY)
 
         s2_spread = held.tile([P, G * WIDTH], U8, name="s2_spread", align_bytes=64)
         gather(nc, s2_spread[:], s2_all, list2, 0, G * WIDTH)
-        s2_dealt = held.tile([P, G * WIDTH], U8, name="s2_dealt", align_bytes=64)
+        s2_dealt = shared.tile([P, G * WIDTH], U8, name="s2_dealt", offset=DEALT_AT, align_bytes=64)
         nc.vector.tensor_copy(
             out=s2_dealt[:].rearrange("q (r d p) -> q d r p", r=G, d=4),
             in_=s2_spread[:].rearrange("q (r p d) -> q d r p", r=G, d=4),
         )
+        warm_up = psum.tile([P, WIDTH], F32, name="warm_up", tag="y_0")
+        zero_codes = s2[:].bitcast(FP8X4)
+        for step in range(WARM_UPS):
+            nc.tensor.matmul_mx(
+                out=warm_up[:],
+                lhsT=zero_codes[:, :P],
+                lhsT_scale=s2_dealt[:, :P],
+                rhs=zero_codes,
+                rhs_scale=s2_dealt[:, :WIDTH],
+                start=True,
+                stop=True,
+            )
         for v in range(4):
             nc.sync.dma_start(
-                out=s2[W2_ROW + v : P : 32, :].bitcast(I32), in_=s2_dealt[S2_ROW + v : P : 4, :].bitcast(I32)
+                out=s2[W2_ROW + v : P : 32, : G * WIDTH].bitcast(I32), in_=s2_dealt[S2_ROW + v : P : 4, :].bitcast(I32)
             )
         s1_early = held.tile([P, (G - 1) * WIDTH], U8, name="s1_early", align_bytes=64)
         gather(nc, s1_early[:], s1_all, list1, 0, (G - 1) * WIDTH)
@@ -114,63 +128,102 @@ def tile_moe_wsel_b_none_p_kernel(
         gather(nc, s1_late[:], s1_all, list1, (G - 1) * WIDTH, WIDTH)
         s1 = [s1_early[:, r * WIDTH : (r + 1) * WIDTH] for r in range(G - 1)] + [s1_late[:]]
 
-        h_grouped = {}
-        for r in range(G):
-            for j in range(HALVES):
-                tokens = slice(j * P, (j + 1) * P)
+        def first_product(r, j):
+            tokens = slice(j * P, (j + 1) * P)
+            if (r, j) == ON_VECTOR:
+                sums = psum.tile([P, WIDTH], F32, name="sums", tag="y_1")
+            else:
                 sums = psum.tile([P, WIDTH], F32, name="sums", tag="sums", bufs=3)
-                nc.tensor.matmul_mx(
-                    out=sums[:],
-                    lhsT=x_codes[:, tokens].bitcast(FP8X4),
-                    lhsT_scale=x_plane[X_ROW:P, tokens],
-                    rhs=w1[r][:].bitcast(FP8X4),
-                    rhs_scale=s1[r],
-                    start=True,
-                    stop=True,
-                )
-                h_rows = held.tile([P, 2, P, 2], BF16, name="h_rows_%d_%d" % (r, j))
-                dealt = sums[:].rearrange("t (p u e) -> t u p e", u=2, e=2)
-                gate_column = gate_cols[:, j, r : r + 1]
-                if (r, j) == ON_VECTOR:
-                    nc.vector.tensor_scalar(out=h_rows[:], in0=dealt, scalar1=gate_column, scalar2=None, op0=MULT)
-                else:
-                    nc.scalar.activation(out=h_rows[:], in_=dealt, func=COPY, scale=gate_column)
-                pairs = h_rows[:].rearrange("t u p e -> t (u p e)").bitcast(F32)
-                turned = psum.tile([P, 2, P], F32, name="turned", tag="turned", bufs=3)
-                for u in range(2):
-                    nc.tensor.transpose(turned[:, u, :], pairs[:, u * P : (u + 1) * P], identity[:])
-                h_grouped[r, j] = held.tile([P, P * 4], BF16, name="h_grouped_%d_%d" % (r, j), align_bytes=64)
-                nc.scalar.copy(
-                    out=h_grouped[r, j][:].bitcast(F32).rearrange("p (t u) -> p t u", u=2),
-                    in_=turned[:].rearrange("p u t -> p t u"),
-                )
+            nc.tensor.matmul_mx(
+                out=sums[:],
+                lhsT=x_codes[:, tokens].bitcast(FP8X4),
+                lhsT_scale=x_plane[X_ROW:P, tokens],
+                rhs=w1[r][:].bitcast(FP8X4),
+                rhs_scale=s1[r],
+                start=True,
+                stop=True,
+            )
+            h_rows = held.tile([P, 2, P, 2], BF16, name="h_rows_%d_%d" % (r, j))
+            dealt = sums[:].rearrange("t (p u e) -> t u p e", u=2, e=2)
+            gate_column = gate_cols[:, HALVES * r + j : HALVES * r + j + 1]
+            if (r, j) == ON_VECTOR:
+                nc.vector.tensor_scalar(out=h_rows[:], in0=dealt, scalar1=gate_column, scalar2=None, op0=MULT)
+            else:
+                nc.scalar.activation(out=h_rows[:], in_=dealt, func=COPY, scale=gate_column)
+            return h_rows
 
-        w2 = []
-        for r in range(G):
-            w2.append(held.tile([P, WIDTH], U32, name="w2_%d" % r, align_bytes=64))
-            gather(nc, w2[r][:].rearrange("q (d p) -> q p d", d=4), w2_all, list2, r * WIDTH, WIDTH)
+        def turn(r, j, h_rows):
+            pairs = h_rows[:].rearrange("t u p e -> t (u p e)").bitcast(F32)
+            ring = "sums" if (r, j) == units[-1] else "turned"
+            turned = psum.tile([P, 2, P], F32, name="turned", tag=ring, bufs=3)
+            for u in range(2):
+                nc.tensor.transpose(turned[:, u, :], pairs[:, u * P : (u + 1) * P], identity[:])
+            if (r, j) == (0, 0):
+                grouped = shared.tile(
+                    [P, P * 4], BF16, name="h_grouped_%d_%d" % (r, j), offset=LAST_W2_AT, align_bytes=64
+                )
+            elif (r, j) in LATE_H_AT:
+                grouped = shared.tile(
+                    [P, P * 4], BF16, name="h_grouped_%d_%d" % (r, j), offset=LATE_H_AT[r, j], align_bytes=64
+                )
+            else:
+                grouped = held.tile([P, P * 4], BF16, name="h_grouped", tag="h_second_and_last", align_bytes=64)
+            nc.scalar.copy(
+                out=grouped[:].bitcast(F32).rearrange("p (t u) -> p t u", u=2),
+                in_=turned[:].rearrange("p u t -> p t u"),
+            )
+            return grouped
 
-        y_sums = [psum.tile([P, 4, P], F32, name="y_sums_%d" % j) for j in range(HALVES)]
-        for r in range(G):
-            for j in range(HALVES):
-                if r == 0:
-                    h_codes = held.tile([P, P], U32, name="h_codes_%d_%d" % (r, j), align_bytes=64)
-                else:
-                    h_codes = shared.tile(
-                        [P, P], U32, name="h_codes_%d_%d" % (r, j), offset=4 * P * (HALVES * r + j), align_bytes=64
-                    )
+        units = [(r, j) for r in range(G) for j in range(HALVES)]
+        h_rows, h_grouped = {}, {}
+        for unit in units:
+            h_rows[unit] = first_product(*unit)
+            if unit != (1, 1):
+                h_grouped[unit] = turn(*unit, h_rows[unit])
+            if unit == (2, 0):
+                h_grouped[1, 1] = turn(1, 1, h_rows[1, 1])
+
+        def gather_w2(r):
+            if r < G - 1:
+                w2 = held.tile([P, WIDTH], U32, name="w2_%d" % r, align_bytes=64)
+            else:
+                w2 = shared.tile([P, WIDTH], U32, name="w2_%d" % r, offset=LAST_W2_AT, align_bytes=64)
+            gather(nc, w2[:].rearrange("q (d p) -> q p d", d=4), w2_all, list2, r * WIDTH, WIDTH)
+            return w2
+
+        def quantise_h(r, j):
+            h_codes = held.tile([P, P], U32, name="h_codes_%d_%d" % (r, j), align_bytes=64)
+            if r == 0:
+                h_plane = shared.tile(
+                    [P, P], U8, name="h_plane_%d_%d" % (r, j), offset=DEALT_AT + P * (1 + j), align_bytes=64
+                )
+            else:
                 h_plane = held.tile([P, P], U8, name="h_plane_%d_%d" % (r, j), align_bytes=64)
-                nc.vector.quantize_mx(out=h_codes[:].bitcast(FP8X4), scales=h_plane[:], in_=h_grouped[r, j][:])
-                for d in range(4):
-                    nc.tensor.matmul_mx(
-                        out=y_sums[j][:, d, :],
-                        lhsT=w2[r][:, d * P : (d + 1) * P].bitcast(FP8X4),
-                        lhsT_scale=s2[W2_ROW:P, r * WIDTH + d * P : r * WIDTH + (d + 1) * P],
-                        rhs=h_codes[:].bitcast(FP8X4),
-                        rhs_scale=h_plane[:],
-                        start=(r == 0 and d == 0),
-                        stop=(r == G - 1 and d == 3),
-                    )
+            nc.vector.quantize_mx(out=h_codes[:].bitcast(FP8X4), scales=h_plane[:], in_=h_grouped[r, j][:])
+            return h_codes, h_plane
+
+        y_sums = [psum.tile([P, 4, P], F32, name="y_sums_%d" % j, tag="y_%d" % j) for j in range(HALVES)]
+        w2 = [gather_w2(r) for r in range(G - 1)]
+
+        def second_product(r, j):
+            h_codes, h_plane = quantise_h(r, j)
+            for d in range(4):
+                nc.tensor.matmul_mx(
+                    out=y_sums[j][:, d, :],
+                    lhsT=w2[r][:, d * P : (d + 1) * P].bitcast(FP8X4),
+                    lhsT_scale=s2[W2_ROW:P, r * WIDTH + d * P : r * WIDTH + (d + 1) * P],
+                    rhs=h_codes[:].bitcast(FP8X4),
+                    rhs_scale=h_plane[:],
+                    start=(r == 0 and d == 0),
+                    stop=(r == G - 1 and d == 3),
+                )
+
+        for j in range(HALVES):
+            second_product(0, j)
+        w2.append(gather_w2(G - 1))
+        for j in range(HALVES):
+            for r in range(1, G):
+                second_product(r, j)
 
         y_grouped = held.tile([P, T, 4], BF16, name="y_grouped", align_bytes=64)
         out_rows = out_0.rearrange("(p d) t -> p d t", d=4)
@@ -182,13 +235,13 @@ def tile_moe_wsel_b_none_p_kernel(
                 nc.vector.tensor_copy(out=y[:], in_=y_sums[j][:])
                 nc.vector.tensor_copy(out=y_grouped[:, tokens, :], in_=regrouped)
             else:
-                nc.scalar.copy(out=y_grouped[:, tokens, :], in_=regrouped)
                 nc.scalar.copy(out=y[:], in_=y_sums[j][:])
+                nc.scalar.copy(out=y_grouped[:, tokens, :], in_=regrouped)
             nc.sync.dma_start(out=out_rows[:, :, tokens], in_=y[:])
 
         y_codes = held.tile([P, T], U32, name="y_codes", align_bytes=64)
         y_plane = held.tile([P, T], U8, name="y_plane", align_bytes=64)
-        for j in reversed(range(HALVES)):
+        for j in range(HALVES):
             tokens = slice(j * P, (j + 1) * P)
             nc.vector.quantize_mx(
                 out=y_codes[:, tokens].bitcast(FP8X4),

@@ -26,7 +26,6 @@ W1_ALL_AT = 4 * COLUMNS
 DEALT_AT = 8 * COLUMNS + 8 * P
 LAST_W2_AT = DEALT_AT + 5 * WIDTH
 LATE_H_AT = {(1, 0): DEALT_AT - 7 * P, (1, 1): DEALT_AT + 3 * P, (2, 0): DEALT_AT + 11 * P}
-WARM_UPS = 3
 ON_VECTOR = (1, 1)
 
 FLOPS = 2 * 2 * G * WIDTH * WIDTH * T
@@ -69,7 +68,7 @@ def tile_moe_wsel_b_none_p_kernel(
         s1_all = held.tile([P, COLUMNS], U8, name="s1_all", align_bytes=64)
         s2_all = held.tile([P, COLUMNS], U8, name="s2_all", align_bytes=64)
         x_plane = held.tile([P, T], U8, name="x_plane", align_bytes=64)
-        s2 = held.tile([P, 4 * WIDTH], U8, name="s2", align_bytes=64)
+        s2 = held.tile([P, G * WIDTH], U8, name="s2", align_bytes=64)
         w1_all = shared.tile([P, COLUMNS], U32, name="w1_all", offset=W1_ALL_AT, align_bytes=64)
         w2_all = shared.tile([P, COLUMNS], U32, name="w2_all", offset=0, align_bytes=64)
 
@@ -102,21 +101,9 @@ def tile_moe_wsel_b_none_p_kernel(
             out=s2_dealt[:].rearrange("q (r d p) -> q d r p", r=G, d=4),
             in_=s2_spread[:].rearrange("q (r p d) -> q d r p", r=G, d=4),
         )
-        warm_up = psum.tile([P, WIDTH], F32, name="warm_up", tag="y_0")
-        zero_codes = s2[:].bitcast(FP8X4)
-        for step in range(WARM_UPS):
-            nc.tensor.matmul_mx(
-                out=warm_up[:],
-                lhsT=zero_codes[:, :P],
-                lhsT_scale=s2_dealt[:, :P],
-                rhs=zero_codes,
-                rhs_scale=s2_dealt[:, :WIDTH],
-                start=True,
-                stop=True,
-            )
         for v in range(4):
             nc.sync.dma_start(
-                out=s2[W2_ROW + v : P : 32, : G * WIDTH].bitcast(I32), in_=s2_dealt[S2_ROW + v : P : 4, :].bitcast(I32)
+                out=s2[W2_ROW + v : P : 32, :].bitcast(I32), in_=s2_dealt[S2_ROW + v : P : 4, :].bitcast(I32)
             )
         s1_early = held.tile([P, (G - 1) * WIDTH], U8, name="s1_early", align_bytes=64)
         gather(nc, s1_early[:], s1_all, list1, 0, (G - 1) * WIDTH)

@@ -76,8 +76,9 @@ def tile_moe_wsel_b_none_p_kernel(
         nc.vector.memset(s2_all[:S2_ROW, :].bitcast(I32), 0)
         nc.vector.memset(x_plane[:].bitcast(I32), 0)
         nc.vector.memset(gate_rows[:], 0.0)
-        make_identity(nc, identity[:])
-        nc.gpsimd.memset(s2[:].bitcast(I32), 0)
+        nc.vector.memset(s2[:].bitcast(I32), 0)
+        nc.vector.memset(identity[:], 0.0)
+        make_identity(nc, identity[:], nomemset=True)
 
         nc.sync.dma_start(out=s2_all[S2_ROW:, :].bitcast(I32), in_=w2_scales[0].bitcast(I32))
         nc.sync.dma_start(list2[:], offs2)
@@ -117,26 +118,29 @@ def tile_moe_wsel_b_none_p_kernel(
 
         def first_product(r, j):
             tokens = slice(j * P, (j + 1) * P)
-            if (r, j) == ON_VECTOR:
-                sums = psum.tile([P, WIDTH], F32, name="sums", tag="y_1")
-            else:
-                sums = psum.tile([P, WIDTH], F32, name="sums", tag="sums", bufs=3)
-            nc.tensor.matmul_mx(
-                out=sums[:],
-                lhsT=x_codes[:, tokens].bitcast(FP8X4),
-                lhsT_scale=x_plane[X_ROW:P, tokens],
-                rhs=w1[r][:].bitcast(FP8X4),
-                rhs_scale=s1[r],
-                start=True,
-                stop=True,
-            )
             h_rows = held.tile([P, 2, P, 2], BF16, name="h_rows_%d_%d" % (r, j))
-            dealt = sums[:].rearrange("t (p u e) -> t u p e", u=2, e=2)
             gate_column = gate_cols[:, HALVES * r + j : HALVES * r + j + 1]
-            if (r, j) == ON_VECTOR:
-                nc.vector.tensor_scalar(out=h_rows[:], in0=dealt, scalar1=gate_column, scalar2=None, op0=MULT)
-            else:
-                nc.scalar.activation(out=h_rows[:], in_=dealt, func=COPY, scale=gate_column)
+            width = WIDTH // 2 if r == 0 else WIDTH
+            for first in range(0, WIDTH, width):
+                if (r, j) == ON_VECTOR:
+                    sums = psum.tile([P, width], F32, name="sums", tag="y_1")
+                else:
+                    sums = psum.tile([P, width], F32, name="sums", tag="sums", bufs=3)
+                nc.tensor.matmul_mx(
+                    out=sums[:],
+                    lhsT=x_codes[:, tokens].bitcast(FP8X4),
+                    lhsT_scale=x_plane[X_ROW:P, tokens],
+                    rhs=w1[r][:, first : first + width].bitcast(FP8X4),
+                    rhs_scale=s1[r][:, first : first + width],
+                    start=True,
+                    stop=True,
+                )
+                part = h_rows[:, :, first // 4 : (first + width) // 4, :]
+                dealt = sums[:].rearrange("t (p u e) -> t u p e", u=2, e=2)
+                if (r, j) == ON_VECTOR:
+                    nc.vector.tensor_scalar(out=part, in0=dealt, scalar1=gate_column, scalar2=None, op0=MULT)
+                else:
+                    nc.scalar.activation(out=part, in_=dealt, func=COPY, scale=gate_column)
             return h_rows
 
         def turn(r, j, h_rows):
@@ -189,20 +193,23 @@ def tile_moe_wsel_b_none_p_kernel(
             nc.vector.quantize_mx(out=h_codes[:].bitcast(FP8X4), scales=h_plane[:], in_=h_grouped[r, j][:])
             return h_codes, h_plane
 
-        y_sums = [psum.tile([P, 4, P], F32, name="y_sums_%d" % j, tag="y_%d" % j) for j in range(HALVES)]
+        y_first = psum.tile([P, 4, P], F32, name="y_first", tag="y_0")
+        y_low = psum.tile([P, 2, P], F32, name="y_low", tag="y_1")
+        y_high = psum.tile([P, 2, P], F32, name="y_high", tag="sums", bufs=3)
+        y_sums = [[y_first[:, d, :] for d in range(4)], [y_low[:, 0, :], y_low[:, 1, :], y_high[:, 0, :], y_high[:, 1, :]]]
         w2 = [gather_w2(r) for r in range(G - 1)]
 
         def second_product(r, j):
             h_codes, h_plane = quantise_h(r, j)
             for d in range(4):
                 nc.tensor.matmul_mx(
-                    out=y_sums[j][:, d, :],
+                    out=y_sums[j][d],
                     lhsT=w2[r][:, d * P : (d + 1) * P].bitcast(FP8X4),
                     lhsT_scale=s2[W2_ROW:P, r * WIDTH + d * P : r * WIDTH + (d + 1) * P],
                     rhs=h_codes[:].bitcast(FP8X4),
                     rhs_scale=h_plane[:],
-                    start=(r == 0 and d == 0),
-                    stop=(r == G - 1 and d == 3),
+                    start=(r == 0 and (d == 0 or (j, d) == (1, 2))),
+                    stop=(r == G - 1 and (d == 3 or (j, d) == (1, 1))),
                 )
 
         for j in range(HALVES):
@@ -214,17 +221,14 @@ def tile_moe_wsel_b_none_p_kernel(
 
         y_grouped = held.tile([P, T, 4], BF16, name="y_grouped", align_bytes=64)
         out_rows = out_0.rearrange("(p d) t -> p d t", d=4)
+        y = [held.tile([P, 4, P], F32, name="y_%d" % j) for j in range(HALVES)]
+        nc.vector.tensor_copy(out=y[0][:], in_=y_first[:])
+        nc.vector.tensor_copy(out=y_grouped[:, :P, :], in_=y_first[:].rearrange("p d t -> p t d"))
+        nc.scalar.copy(out=y[1][:, :2, :], in_=y_low[:])
+        nc.scalar.copy(out=y[1][:, 2:, :], in_=y_high[:])
+        nc.vector.tensor_copy(out=y_grouped[:, P:, :], in_=y[1][:].rearrange("p d t -> p t d"))
         for j in range(HALVES):
-            tokens = slice(j * P, (j + 1) * P)
-            y = held.tile([P, 4, P], F32, name="y_%d" % j)
-            regrouped = y_sums[j][:].rearrange("p d t -> p t d")
-            if j == 0:
-                nc.vector.tensor_copy(out=y[:], in_=y_sums[j][:])
-                nc.vector.tensor_copy(out=y_grouped[:, tokens, :], in_=regrouped)
-            else:
-                nc.scalar.copy(out=y[:], in_=y_sums[j][:])
-                nc.scalar.copy(out=y_grouped[:, tokens, :], in_=regrouped)
-            nc.sync.dma_start(out=out_rows[:, :, tokens], in_=y[:])
+            nc.sync.dma_start(out=out_rows[:, :, j * P : (j + 1) * P], in_=y[j][:])
 
         y_codes = held.tile([P, T], U32, name="y_codes", align_bytes=64)
         y_plane = held.tile([P, T], U8, name="y_plane", align_bytes=64)

@@ -17,16 +17,21 @@ P = 128
 T = 256
 G = 3
 WIDTH = 512
+HALF = WIDTH // 2
 COLUMNS = 3072
 HALVES = T // P
 PER_COLUMN = 16
-X_ROW, W1_ROW, W2_ROW = 8, 0, 4
+X_ROW, W2_ROW = 8, 4
 S2_ROW = P - 16
-W1_ALL_AT = 4 * COLUMNS
-DEALT_AT = 8 * COLUMNS + 8 * P
-LAST_W2_AT = DEALT_AT + 5 * WIDTH
-LATE_H_AT = {(1, 0): DEALT_AT - 7 * P, (1, 1): DEALT_AT + 3 * P, (2, 0): DEALT_AT + 11 * P}
-ON_VECTOR = (1, 1)
+DEALT_AT = 7 * P
+LATE_H_AT = {(2, 0): 0, (1, 1): DEALT_AT + 2 * P}
+LATE_PLANE_AT = DEALT_AT + P
+LAST_W2_AT = DEALT_AT + 10 * P
+GATE_ROWS_AT = LAST_W2_AT + 4 * WIDTH
+ON_VECTOR = (1, 0)
+SUMS_BANK = {(0, 0, 0): 0, (0, 1, 0): 1, (0, 0, 1): 2, (0, 1, 1): 3, (1, 0): 4, (1, 1): 3, (2, 0): 0, (2, 1): 3}
+TURNED_BANK = {(0, 0): 0, (0, 1): 1, (1, 0): 1, (1, 1): 2, (2, 0): 0, (2, 1): 0}
+Y_BANK = (6, 7)
 
 FLOPS = 2 * 2 * G * WIDTH * WIDTH * T
 
@@ -43,11 +48,8 @@ def load_scale_rows(nc, plane, scales, first_row):
         nc.sync.dma_start(out=plane[first_row + v : P : 32, :].bitcast(I32), in_=rows[v:16:4, :])
 
 
-def load_words(nc, tile, words, first, last):
-    nc.sync.dma_start(
-        out=tile[:, first:last].bitcast(I32),
-        in_=words[0].rearrange("p m d -> p (m d)").bitcast(I32)[:, first:last],
-    )
+def load_words(nc, tile, words):
+    nc.sync.dma_start(out=tile[:].bitcast(I32), in_=words[0].rearrange("p m d -> p (m d)").bitcast(I32))
 
 
 def tile_moe_wsel_b_none_p_kernel(
@@ -59,18 +61,21 @@ def tile_moe_wsel_b_none_p_kernel(
         shared = ctx.enter_context(tc.tile_pool(name="shared", bufs=1))
         psum = ctx.enter_context(tc.psum_pool(name="psum", bufs=1))
 
+        def bank(number, shape, name):
+            return psum.tile(shape, F32, name=name, tag="bank_%d" % number)
+
         list1 = held.tile([P, G * WIDTH // PER_COLUMN], U16, name="list1")
         list2 = held.tile([P, G * WIDTH // PER_COLUMN], U16, name="list2")
         x_codes = held.tile([P, T], U32, name="x_codes", align_bytes=64)
-        gate_rows = held.tile([P, P], F32, name="gate_rows")
+        gate_rows = shared.tile([P, P], F32, name="gate_rows", offset=GATE_ROWS_AT, align_bytes=64)
         gate_cols = held.tile([P, G * HALVES], F32, name="gate_cols")
         identity = held.tile([P, P], F32, name="identity")
         s1_all = held.tile([P, COLUMNS], U8, name="s1_all", align_bytes=64)
         s2_all = held.tile([P, COLUMNS], U8, name="s2_all", align_bytes=64)
         x_plane = held.tile([P, T], U8, name="x_plane", align_bytes=64)
         s2 = held.tile([P, G * WIDTH], U8, name="s2", align_bytes=64)
-        w1_all = shared.tile([P, COLUMNS], U32, name="w1_all", offset=W1_ALL_AT, align_bytes=64)
-        w2_all = shared.tile([P, COLUMNS], U32, name="w2_all", offset=0, align_bytes=64)
+        w1_all = held.tile([P, COLUMNS], U32, name="w1_all", align_bytes=64)
+        w2_all = held.tile([P, COLUMNS], U32, name="w2_all", align_bytes=64)
 
         nc.vector.memset(s1_all[:].bitcast(I32), 0)
         nc.vector.memset(s2_all[:S2_ROW, :].bitcast(I32), 0)
@@ -83,162 +88,178 @@ def tile_moe_wsel_b_none_p_kernel(
         nc.sync.dma_start(out=s2_all[S2_ROW:, :].bitcast(I32), in_=w2_scales[0].bitcast(I32))
         nc.sync.dma_start(list2[:], offs2)
         nc.sync.dma_start(list1[:], offs)
-        load_scale_rows(nc, s1_all, w1_scales, W1_ROW)
-        load_words(nc, w1_all, w1_words, 0, COLUMNS)
+        load_scale_rows(nc, s1_all, w1_scales, 0)
+        load_words(nc, w1_all, w1_words)
         gate_halves = gate.rearrange("r p (j c) -> (r p j) c", c=P)
         nc.sync.dma_start(out=gate_rows[: G * HALVES, :], in_=gate_halves[0 : G * HALVES * (P + 1) - P : P + 1, :])
-        load_words(nc, x_codes, x_words, 0, T)
+        load_words(nc, x_codes, x_words)
         load_scale_rows(nc, x_plane, x_scales, X_ROW)
-        load_words(nc, w2_all, w2_words, 0, COLUMNS)
+        load_words(nc, w2_all, w2_words)
 
-        gate_bank = psum.tile([P, P], F32, name="gate_bank", tag="turned", bufs=3)
+        gate_bank = bank(Y_BANK[0], [P, P], "gate_bank")
         nc.tensor.transpose(gate_bank[:], gate_rows[:], identity[:])
         nc.scalar.activation(out=gate_cols[:], in_=gate_bank[:, : G * HALVES], func=COPY)
 
-        s2_spread = held.tile([P, G * WIDTH], U8, name="s2_spread", align_bytes=64)
-        gather(nc, s2_spread[:], s2_all, list2, 0, G * WIDTH)
         s2_dealt = shared.tile([P, G * WIDTH], U8, name="s2_dealt", offset=DEALT_AT, align_bytes=64)
-        nc.vector.tensor_copy(
-            out=s2_dealt[:].rearrange("q (r d p) -> q d r p", r=G, d=4),
-            in_=s2_spread[:].rearrange("q (r p d) -> q d r p", r=G, d=4),
-        )
+        s2_spread = held.tile([P, G * WIDTH], U8, name="s2_spread", align_bytes=64)
+        parts = ((0, G - 1), (G - 1, G))
+        for first, last in parts:
+            gather(nc, s2_spread[:, first * WIDTH : last * WIDTH], s2_all, list2, first * WIDTH, (last - first) * WIDTH)
+        for first, last in parts:
+            chosen = slice(first * WIDTH, last * WIDTH)
+            nc.vector.tensor_copy(
+                out=s2_dealt[:, chosen].rearrange("q (r d p) -> q d r p", r=last - first, d=4),
+                in_=s2_spread[:, chosen].rearrange("q (r p d) -> q d r p", r=last - first, d=4),
+            )
         for v in range(4):
             nc.sync.dma_start(
                 out=s2[W2_ROW + v : P : 32, :].bitcast(I32), in_=s2_dealt[S2_ROW + v : P : 4, :].bitcast(I32)
             )
         s1_early = held.tile([P, (G - 1) * WIDTH], U8, name="s1_early", align_bytes=64)
         gather(nc, s1_early[:], s1_all, list1, 0, (G - 1) * WIDTH)
-        w1 = []
-        for r in range(G):
-            w1.append(held.tile([P, WIDTH], U32, name="w1_%d" % r, align_bytes=64))
-            gather(nc, w1[r][:], w1_all, list1, r * WIDTH, WIDTH)
-        s1_late = shared.tile([P, WIDTH], U8, name="s1_late", offset=W1_ALL_AT, align_bytes=64)
+        w1 = held.tile([P, G * WIDTH], U32, name="w1", align_bytes=64)
+        for first, count in ((0, HALF), (HALF, HALF), (WIDTH, WIDTH), (2 * WIDTH, WIDTH)):
+            gather(nc, w1[:, first : first + count], w1_all, list1, first, count)
+        s1_late = shared.tile([P, WIDTH], U8, name="s1_late", offset=GATE_ROWS_AT, align_bytes=64)
         gather(nc, s1_late[:], s1_all, list1, (G - 1) * WIDTH, WIDTH)
-        s1 = [s1_early[:, r * WIDTH : (r + 1) * WIDTH] for r in range(G - 1)] + [s1_late[:]]
-
-        def first_product(r, j):
-            tokens = slice(j * P, (j + 1) * P)
-            h_rows = held.tile([P, 2, P, 2], BF16, name="h_rows_%d_%d" % (r, j))
-            gate_column = gate_cols[:, HALVES * r + j : HALVES * r + j + 1]
-            width = WIDTH // 2 if r == 0 else WIDTH
-            for first in range(0, WIDTH, width):
-                if (r, j) == ON_VECTOR:
-                    sums = psum.tile([P, width], F32, name="sums", tag="y_1")
-                else:
-                    sums = psum.tile([P, width], F32, name="sums", tag="sums", bufs=3)
-                nc.tensor.matmul_mx(
-                    out=sums[:],
-                    lhsT=x_codes[:, tokens].bitcast(FP8X4),
-                    lhsT_scale=x_plane[X_ROW:P, tokens],
-                    rhs=w1[r][:, first : first + width].bitcast(FP8X4),
-                    rhs_scale=s1[r][:, first : first + width],
-                    start=True,
-                    stop=True,
-                )
-                part = h_rows[:, :, first // 4 : (first + width) // 4, :]
-                dealt = sums[:].rearrange("t (p u e) -> t u p e", u=2, e=2)
-                if (r, j) == ON_VECTOR:
-                    nc.vector.tensor_scalar(out=part, in0=dealt, scalar1=gate_column, scalar2=None, op0=MULT)
-                else:
-                    nc.scalar.activation(out=part, in_=dealt, func=COPY, scale=gate_column)
-            return h_rows
-
-        def turn(r, j, h_rows):
-            pairs = h_rows[:].rearrange("t u p e -> t (u p e)").bitcast(F32)
-            ring = "sums" if (r, j) == units[-1] else "turned"
-            turned = psum.tile([P, 2, P], F32, name="turned", tag=ring, bufs=3)
-            for u in range(2):
-                nc.tensor.transpose(turned[:, u, :], pairs[:, u * P : (u + 1) * P], identity[:])
-            if (r, j) == (0, 0):
-                grouped = shared.tile(
-                    [P, P * 4], BF16, name="h_grouped_%d_%d" % (r, j), offset=LAST_W2_AT, align_bytes=64
-                )
-            elif (r, j) in LATE_H_AT:
-                grouped = shared.tile(
-                    [P, P * 4], BF16, name="h_grouped_%d_%d" % (r, j), offset=LATE_H_AT[r, j], align_bytes=64
-                )
-            else:
-                grouped = held.tile([P, P * 4], BF16, name="h_grouped", tag="h_second_and_last", align_bytes=64)
-            nc.scalar.copy(
-                out=grouped[:].bitcast(F32).rearrange("p (t u) -> p t u", u=2),
-                in_=turned[:].rearrange("p u t -> p t u"),
-            )
-            return grouped
 
         units = [(r, j) for r in range(G) for j in range(HALVES)]
-        h_rows, h_grouped = {}, {}
-        for unit in units:
-            h_rows[unit] = first_product(*unit)
-            if unit != (1, 1):
-                h_grouped[unit] = turn(*unit, h_rows[unit])
-            if unit == (2, 0):
-                h_grouped[1, 1] = turn(1, 1, h_rows[1, 1])
+        h_rows = {unit: held.tile([P, 2, P, 2], BF16, name="h_rows_%d_%d" % unit) for unit in units}
+        sums, turned, h_grouped, h_codes, h_plane = {}, {}, {}, {}, {}
+
+        def columns(piece):
+            return (piece[2] * HALF, HALF) if len(piece) == 3 else (0, WIDTH)
+
+        def first_product(*piece):
+            r, j = piece[:2]
+            first, width = columns(piece)
+            tokens = slice(j * P, (j + 1) * P)
+            chosen = slice(r * WIDTH + first, r * WIDTH + first + width)
+            sums[piece] = bank(SUMS_BANK[piece], [P, width], "sums")
+            nc.tensor.matmul_mx(
+                out=sums[piece][:],
+                lhsT=x_codes[:, tokens].bitcast(FP8X4),
+                lhsT_scale=x_plane[X_ROW:P, tokens],
+                rhs=w1[:, chosen].bitcast(FP8X4),
+                rhs_scale=s1_early[:, chosen] if r < G - 1 else s1_late[:],
+                start=True,
+                stop=True,
+            )
+
+        def gate_and_round(*piece):
+            r, j = piece[:2]
+            first, width = columns(piece)
+            gate_column = gate_cols[:, HALVES * r + j : HALVES * r + j + 1]
+            part = h_rows[r, j][:, :, first // 4 : (first + width) // 4, :]
+            dealt = sums[piece][:].rearrange("t (p u e) -> t u p e", u=2, e=2)
+            if (r, j) == ON_VECTOR:
+                nc.vector.tensor_scalar(out=part, in0=dealt, scalar1=gate_column, scalar2=None, op0=MULT)
+            else:
+                nc.scalar.activation(out=part, in_=dealt, func=COPY, scale=gate_column)
+
+        def turn(*unit):
+            pairs = h_rows[unit][:].rearrange("t u p e -> t (u p e)").bitcast(F32)
+            turned[unit] = bank(TURNED_BANK[unit], [P, 2, P], "turned")
+            for u in range(2):
+                nc.tensor.transpose(turned[unit][:, u, :], pairs[:, u * P : (u + 1) * P], identity[:])
+
+        def regroup(*unit):
+            name = "h_grouped_%d_%d" % unit
+            if unit in LATE_H_AT:
+                h_grouped[unit] = shared.tile([P, P * 4], BF16, name=name, offset=LATE_H_AT[unit], align_bytes=64)
+            else:
+                h_grouped[unit] = held.tile([P, P * 4], BF16, name=name, align_bytes=64)
+            nc.scalar.copy(
+                out=h_grouped[unit][:].bitcast(F32).rearrange("p (t u) -> p t u", u=2),
+                in_=turned[unit][:].rearrange("p u t -> p t u"),
+            )
+
+        def quantise_h(*unit):
+            h_codes[unit] = held.tile([P, P], U32, name="h_codes_%d_%d" % unit, align_bytes=64)
+            name = "h_plane_%d_%d" % unit
+            if unit == (1, 0):
+                h_plane[unit] = shared.tile([P, P], U8, name=name, offset=LATE_PLANE_AT, align_bytes=64)
+            else:
+                h_plane[unit] = held.tile([P, P], U8, name=name, align_bytes=64)
+            nc.vector.quantize_mx(out=h_codes[unit][:].bitcast(FP8X4), scales=h_plane[unit][:], in_=h_grouped[unit][:])
+
+        w2 = {}
 
         def gather_w2(r):
             if r < G - 1:
-                w2 = held.tile([P, WIDTH], U32, name="w2_%d" % r, align_bytes=64)
+                w2[r] = held.tile([P, WIDTH], U32, name="w2_%d" % r, align_bytes=64)
             else:
-                w2 = shared.tile([P, WIDTH], U32, name="w2_%d" % r, offset=LAST_W2_AT, align_bytes=64)
-            gather(nc, w2[:].rearrange("q (d p) -> q p d", d=4), w2_all, list2, r * WIDTH, WIDTH)
-            return w2
+                w2[r] = shared.tile([P, WIDTH], U32, name="w2_%d" % r, offset=LAST_W2_AT, align_bytes=64)
+            gather(nc, w2[r][:].rearrange("q (d p) -> q p d", d=4), w2_all, list2, r * WIDTH, WIDTH)
 
-        def quantise_h(r, j):
-            h_codes = held.tile([P, P], U32, name="h_codes_%d_%d" % (r, j), align_bytes=64)
-            if r == 0:
-                h_plane = shared.tile(
-                    [P, P], U8, name="h_plane_%d_%d" % (r, j), offset=DEALT_AT + P * (1 + j), align_bytes=64
-                )
-            else:
-                h_plane = held.tile([P, P], U8, name="h_plane_%d_%d" % (r, j), align_bytes=64)
-            nc.vector.quantize_mx(out=h_codes[:].bitcast(FP8X4), scales=h_plane[:], in_=h_grouped[r, j][:])
-            return h_codes, h_plane
-
-        y_first = psum.tile([P, 4, P], F32, name="y_first", tag="y_0")
-        y_low = psum.tile([P, 2, P], F32, name="y_low", tag="y_1")
-        y_high = psum.tile([P, 2, P], F32, name="y_high", tag="sums", bufs=3)
-        y_sums = [[y_first[:, d, :] for d in range(4)], [y_low[:, 0, :], y_low[:, 1, :], y_high[:, 0, :], y_high[:, 1, :]]]
-        w2 = [gather_w2(r) for r in range(G - 1)]
+        y_sums = [bank(Y_BANK[j], [P, 4, P], "y_sums") for j in range(HALVES)]
 
         def second_product(r, j):
-            h_codes, h_plane = quantise_h(r, j)
             for d in range(4):
                 nc.tensor.matmul_mx(
-                    out=y_sums[j][d],
+                    out=y_sums[j][:, d, :],
                     lhsT=w2[r][:, d * P : (d + 1) * P].bitcast(FP8X4),
                     lhsT_scale=s2[W2_ROW:P, r * WIDTH + d * P : r * WIDTH + (d + 1) * P],
-                    rhs=h_codes[:].bitcast(FP8X4),
-                    rhs_scale=h_plane[:],
-                    start=(r == 0 and (d == 0 or (j, d) == (1, 2))),
-                    stop=(r == G - 1 and (d == 3 or (j, d) == (1, 1))),
+                    rhs=h_codes[r, j][:].bitcast(FP8X4),
+                    rhs_scale=h_plane[r, j][:],
+                    start=(r == 0 and d == 0),
+                    stop=(r == G - 1 and d == 3),
                 )
 
+        for c in range(2):
+            for j in range(HALVES):
+                first_product(0, j, c)
+                gate_and_round(0, j, c)
+        first_product(1, 0)
+        gate_and_round(1, 0)
+        for j in range(HALVES):
+            turn(0, j)
+            regroup(0, j)
+            quantise_h(0, j)
+        for unit in ((1, 1), (2, 0)):
+            first_product(*unit)
+            gate_and_round(*unit)
+        turn(1, 0)
+        regroup(1, 0)
+        first_product(2, 1)
+        gate_and_round(2, 1)
+        turn(1, 1)
+        turn(2, 0)
+        regroup(2, 0)
+        regroup(1, 1)
+        gather_w2(0)
+        gather_w2(1)
         for j in range(HALVES):
             second_product(0, j)
-        w2.append(gather_w2(G - 1))
-        for j in range(HALVES):
-            for r in range(1, G):
-                second_product(r, j)
+        turn(2, 1)
+        regroup(2, 1)
+        quantise_h(1, 0)
+        second_product(1, 0)
+        gather_w2(2)
+        for unit in ((2, 0), (1, 1), (2, 1)):
+            quantise_h(*unit)
+            second_product(*unit)
 
-        y_grouped = held.tile([P, T, 4], BF16, name="y_grouped", align_bytes=64)
         out_rows = out_0.rearrange("(p d) t -> p d t", d=4)
         y = [held.tile([P, 4, P], F32, name="y_%d" % j) for j in range(HALVES)]
-        nc.vector.tensor_copy(out=y[0][:], in_=y_first[:])
-        nc.vector.tensor_copy(out=y_grouped[:, :P, :], in_=y_first[:].rearrange("p d t -> p t d"))
-        nc.scalar.copy(out=y[1][:, :2, :], in_=y_low[:])
-        nc.scalar.copy(out=y[1][:, 2:, :], in_=y_high[:])
-        nc.vector.tensor_copy(out=y_grouped[:, P:, :], in_=y[1][:].rearrange("p d t -> p t d"))
-        for j in range(HALVES):
-            nc.sync.dma_start(out=out_rows[:, :, j * P : (j + 1) * P], in_=y[j][:])
-
+        y_grouped = [held.tile([P, P, 4], BF16, name="y_grouped_%d" % j, align_bytes=64) for j in range(HALVES)]
         y_codes = held.tile([P, T], U32, name="y_codes", align_bytes=64)
         y_plane = held.tile([P, T], U8, name="y_plane", align_bytes=64)
+        nc.scalar.copy(out=y[0][:], in_=y_sums[0][:])
+        nc.sync.dma_start(out=out_rows[:, :, :P], in_=y[0][:])
+        nc.vector.tensor_copy(out=y_grouped[0][:], in_=y[0][:].rearrange("p d t -> p t d"))
+        nc.scalar.copy(out=y_grouped[1][:], in_=y_sums[1][:].rearrange("p d t -> p t d"))
         for j in range(HALVES):
             tokens = slice(j * P, (j + 1) * P)
             nc.vector.quantize_mx(
                 out=y_codes[:, tokens].bitcast(FP8X4),
                 scales=y_plane[:, tokens],
-                in_=y_grouped[:, tokens, :].rearrange("p t d -> p (t d)"),
+                in_=y_grouped[j][:].rearrange("p t d -> p (t d)"),
             )
+        for pair, queue in enumerate((nc.sync, nc.scalar)):
+            rows = slice(2 * pair, 2 * pair + 2)
+            nc.scalar.copy(out=y[1][:, rows, :], in_=y_sums[1][:, rows, :])
+            queue.dma_start(out=out_rows[:, rows, P:], in_=y[1][:, rows, :])
         nc.sync.dma_start(
             out=out_1[0].rearrange("p t d -> p (t d)").bitcast(I32), in_=y_codes[:].bitcast(I32)
         )

@@ -31,7 +31,7 @@ GATE_ROWS_AT = LAST_W2_AT + 4 * WIDTH
 ON_VECTOR = (1, 0)
 SUMS_BANK = {(0, 0, 0): 0, (0, 1, 0): 1, (0, 0, 1): 2, (0, 1, 1): 3, (1, 0): 4, (1, 1): 3, (2, 0): 0, (2, 1): 3}
 TURNED_BANK = {(0, 0): 0, (0, 1): 1, (1, 0): 1, (1, 1): 2, (2, 0): 0, (2, 1): 0}
-Y_BANK = (6, 7)
+Y_BANK = (6, 7, 5)
 
 FLOPS = 2 * 2 * G * WIDTH * WIDTH * T
 
@@ -192,18 +192,20 @@ def tile_moe_wsel_b_none_p_kernel(
                 w2[r] = shared.tile([P, WIDTH], U32, name="w2_%d" % r, offset=LAST_W2_AT, align_bytes=64)
             gather(nc, w2[r][:].rearrange("q (d p) -> q p d", d=4), w2_all, list2, r * WIDTH, WIDTH)
 
-        y_sums = [bank(Y_BANK[j], [P, 4, P], "y_sums") for j in range(HALVES)]
+        y_first = bank(Y_BANK[0], [P, 4, P], "y_first")
+        y_pairs = [bank(Y_BANK[1 + pair], [P, 2, P], "y_pair") for pair in range(2)]
 
         def second_product(r, j):
+            group = 4 if j == 0 else 2
             for d in range(4):
                 nc.tensor.matmul_mx(
-                    out=y_sums[j][:, d, :],
+                    out=y_first[:, d, :] if j == 0 else y_pairs[d // 2][:, d % 2, :],
                     lhsT=w2[r][:, d * P : (d + 1) * P].bitcast(FP8X4),
                     lhsT_scale=s2[W2_ROW:P, r * WIDTH + d * P : r * WIDTH + (d + 1) * P],
                     rhs=h_codes[r, j][:].bitcast(FP8X4),
                     rhs_scale=h_plane[r, j][:],
-                    start=(r == 0 and d == 0),
-                    stop=(r == G - 1 and d == 3),
+                    start=(r == 0 and d % group == 0),
+                    stop=(r == G - 1 and d % group == group - 1),
                 )
 
         for c in range(2):
@@ -245,10 +247,13 @@ def tile_moe_wsel_b_none_p_kernel(
         y_grouped = [held.tile([P, P, 4], BF16, name="y_grouped_%d" % j, align_bytes=64) for j in range(HALVES)]
         y_codes = held.tile([P, T], U32, name="y_codes", align_bytes=64)
         y_plane = held.tile([P, T], U8, name="y_plane", align_bytes=64)
-        nc.scalar.copy(out=y[0][:], in_=y_sums[0][:])
-        nc.sync.dma_start(out=out_rows[:, :, :P], in_=y[0][:])
-        nc.vector.tensor_copy(out=y_grouped[0][:], in_=y[0][:].rearrange("p d t -> p t d"))
-        nc.scalar.copy(out=y_grouped[1][:], in_=y_sums[1][:].rearrange("p d t -> p t d"))
+        nc.vector.tensor_copy(out=y[0][:], in_=y_first[:])
+        nc.vector.tensor_copy(out=y_grouped[0][:], in_=y_first[:].rearrange("p d t -> p t d"))
+        for pair in range(2):
+            nc.scalar.copy(out=y[1][:, 2 * pair : 2 * pair + 2, :], in_=y_pairs[pair][:])
+        nc.vector.tensor_copy(out=y_grouped[1][:], in_=y[1][:].rearrange("p d t -> p t d"))
+        for j in range(HALVES):
+            nc.sync.dma_start(out=out_rows[:, :, j * P : (j + 1) * P], in_=y[j][:])
         for j in range(HALVES):
             tokens = slice(j * P, (j + 1) * P)
             nc.vector.quantize_mx(
@@ -256,10 +261,6 @@ def tile_moe_wsel_b_none_p_kernel(
                 scales=y_plane[:, tokens],
                 in_=y_grouped[j][:].rearrange("p t d -> p (t d)"),
             )
-        for pair, queue in enumerate((nc.sync, nc.scalar)):
-            rows = slice(2 * pair, 2 * pair + 2)
-            nc.scalar.copy(out=y[1][:, rows, :], in_=y_sums[1][:, rows, :])
-            queue.dma_start(out=out_rows[:, rows, P:], in_=y[1][:, rows, :])
         nc.sync.dma_start(
             out=out_1[0].rearrange("p t d -> p (t d)").bitcast(I32), in_=y_codes[:].bitcast(I32)
         )

@@ -31,7 +31,7 @@ GATE_ROWS_AT = LAST_W2_AT + 4 * WIDTH
 ON_VECTOR = (1, 0)
 SUMS_BANK = {(0, 0, 0): 0, (0, 1, 0): 1, (0, 0, 1): 2, (0, 1, 1): 3, (1, 0): 4, (1, 1): 3, (2, 0): 0, (2, 1): 3}
 TURNED_BANK = {(0, 0): 0, (0, 1): 1, (1, 0): 1, (1, 1): 2, (2, 0): 0, (2, 1): 0}
-Y_BANK = (6, 7, 5)
+Y_BANK = ((6, 4), (7, 5))
 
 FLOPS = 2 * 2 * G * WIDTH * WIDTH * T
 
@@ -96,7 +96,7 @@ def tile_moe_wsel_b_none_p_kernel(
         load_scale_rows(nc, x_plane, x_scales, X_ROW)
         load_words(nc, w2_all, w2_words)
 
-        gate_bank = bank(Y_BANK[0], [P, P], "gate_bank")
+        gate_bank = bank(Y_BANK[0][0], [P, P], "gate_bank")
         nc.tensor.transpose(gate_bank[:], gate_rows[:], identity[:])
         nc.scalar.activation(out=gate_cols[:], in_=gate_bank[:, : G * HALVES], func=COPY)
 
@@ -192,20 +192,18 @@ def tile_moe_wsel_b_none_p_kernel(
                 w2[r] = shared.tile([P, WIDTH], U32, name="w2_%d" % r, offset=LAST_W2_AT, align_bytes=64)
             gather(nc, w2[r][:].rearrange("q (d p) -> q p d", d=4), w2_all, list2, r * WIDTH, WIDTH)
 
-        y_first = bank(Y_BANK[0], [P, 4, P], "y_first")
-        y_pairs = [bank(Y_BANK[1 + pair], [P, 2, P], "y_pair") for pair in range(2)]
+        y_sums = [[bank(Y_BANK[j][pair], [P, 2, P], "y_sums") for pair in range(2)] for j in range(HALVES)]
 
         def second_product(r, j):
-            group = 4 if j == 0 else 2
             for d in range(4):
                 nc.tensor.matmul_mx(
-                    out=y_first[:, d, :] if j == 0 else y_pairs[d // 2][:, d % 2, :],
+                    out=y_sums[j][d // 2][:, d % 2, :],
                     lhsT=w2[r][:, d * P : (d + 1) * P].bitcast(FP8X4),
                     lhsT_scale=s2[W2_ROW:P, r * WIDTH + d * P : r * WIDTH + (d + 1) * P],
                     rhs=h_codes[r, j][:].bitcast(FP8X4),
                     rhs_scale=h_plane[r, j][:],
-                    start=(r == 0 and d % group == 0),
-                    stop=(r == G - 1 and d % group == group - 1),
+                    start=(r == 0 and d % 2 == 0),
+                    stop=(r == G - 1 and d % 2 == 1),
                 )
 
         for c in range(2):
@@ -243,28 +241,38 @@ def tile_moe_wsel_b_none_p_kernel(
             second_product(*unit)
 
         out_rows = out_0.rearrange("(p d) t -> p d t", d=4)
+        out_words = out_1[0].rearrange("p t d -> p (t d)").bitcast(I32)
         y = [held.tile([P, 4, P], F32, name="y_%d" % j) for j in range(HALVES)]
         y_grouped = [held.tile([P, P, 4], BF16, name="y_grouped_%d" % j, align_bytes=64) for j in range(HALVES)]
         y_codes = held.tile([P, T], U32, name="y_codes", align_bytes=64)
         y_plane = held.tile([P, T], U8, name="y_plane", align_bytes=64)
-        nc.vector.tensor_copy(out=y[0][:], in_=y_first[:])
-        nc.vector.tensor_copy(out=y_grouped[0][:], in_=y_first[:].rearrange("p d t -> p t d"))
-        for pair in range(2):
-            nc.scalar.copy(out=y[1][:, 2 * pair : 2 * pair + 2, :], in_=y_pairs[pair][:])
-        nc.vector.tensor_copy(out=y_grouped[1][:], in_=y[1][:].rearrange("p d t -> p t d"))
-        for j in range(HALVES):
+
+        def leave_psum(j):
+            nc.scalar.copy(out=y[j][:, :2, :], in_=y_sums[j][0][:])
+            if j == 0:
+                nc.vector.tensor_copy(out=y[j][:, 2:, :], in_=y_sums[j][1][:])
+            else:
+                nc.scalar.copy(out=y[j][:, 2:, :], in_=y_sums[j][1][:])
             nc.sync.dma_start(out=out_rows[:, :, j * P : (j + 1) * P], in_=y[j][:])
-        for j in range(HALVES):
+
+        def round_y(j):
+            nc.vector.tensor_copy(out=y_grouped[j][:], in_=y[j][:].rearrange("p d t -> p t d"))
+
+        def quantise_y(j):
             tokens = slice(j * P, (j + 1) * P)
             nc.vector.quantize_mx(
                 out=y_codes[:, tokens].bitcast(FP8X4),
                 scales=y_plane[:, tokens],
                 in_=y_grouped[j][:].rearrange("p t d -> p (t d)"),
             )
-        nc.sync.dma_start(
-            out=out_1[0].rearrange("p t d -> p (t d)").bitcast(I32), in_=y_codes[:].bitcast(I32)
-        )
+            nc.sync.dma_start(out=out_words[:, tokens], in_=y_codes[:, tokens].bitcast(I32))
+
+        for j in range(HALVES):
+            leave_psum(j)
+            round_y(j)
+        for j in range(HALVES):
+            quantise_y(j)
         scale_rows = out_2[0].bitcast(I32)
         for v in range(4):
-            queue = nc.scalar if v < 2 else nc.sync
+            queue = nc.scalar if v < 3 else nc.sync
             queue.dma_start(out=scale_rows[v:16:4, :], in_=y_plane[v:P:32, :].bitcast(I32))

@@ -265,14 +265,14 @@ def tile_moe_wsel_b_none_p_kernel(
                 scales=y_plane[:, tokens],
                 in_=y_grouped[j][:].rearrange("p t d -> p (t d)"),
             )
-            nc.sync.dma_start(out=out_words[:, tokens], in_=y_codes[:, tokens].bitcast(I32))
 
         for j in range(HALVES):
             leave_psum(j)
             round_y(j)
         for j in range(HALVES):
             quantise_y(j)
+        nc.sync.dma_start(out=out_words, in_=y_codes[:].bitcast(I32))
         scale_rows = out_2[0].bitcast(I32)
         for v in range(4):
-            queue = nc.scalar if v < 3 else nc.sync
+            queue = nc.scalar if v < 2 else nc.sync
             queue.dma_start(out=scale_rows[v:16:4, :], in_=y_plane[v:P:32, :].bitcast(I32))

@@ -28,8 +28,8 @@ LATE_H_AT = {(2, 0): 0, (1, 1): DEALT_AT + 2 * P}
 LATE_PLANE_AT = DEALT_AT + P
 LAST_W2_AT = DEALT_AT + 10 * P
 GATE_ROWS_AT = LAST_W2_AT + 4 * WIDTH
-ON_VECTOR = (1, 0)
-SUMS_BANK = {(0, 0, 0): 0, (0, 1, 0): 1, (0, 0, 1): 2, (0, 1, 1): 3, (1, 0): 4, (1, 1): 3, (2, 0): 0, (2, 1): 3}
+ON_VECTOR = ((1, 0, 1), (1, 1, 0))
+SUMS_BANK = {(0, 0, 0): 0, (0, 1, 0): 1, (0, 0, 1): 2, (0, 1, 1): 3, (1, 0, 0): 4, (1, 0, 1): 5, (1, 1, 0): 3, (1, 1, 1): 4, (2, 0): 0, (2, 1): 3}
 TURNED_BANK = {(0, 0): 0, (0, 1): 1, (1, 0): 1, (1, 1): 2, (2, 0): 0, (2, 1): 0}
 Y_BANK = ((6, 4), (7, 5))
 
@@ -152,7 +152,7 @@ def tile_moe_wsel_b_none_p_kernel(
             gate_column = gate_cols[:, HALVES * r + j : HALVES * r + j + 1]
             part = h_rows[r, j][:, :, first // 4 : (first + width) // 4, :]
             dealt = sums[piece][:].rearrange("t (p u e) -> t u p e", u=2, e=2)
-            if (r, j) == ON_VECTOR:
+            if piece in ON_VECTOR:
                 nc.vector.tensor_scalar(out=part, in0=dealt, scalar1=gate_column, scalar2=None, op0=MULT)
             else:
                 nc.scalar.activation(out=part, in_=dealt, func=COPY, scale=gate_column)
@@ -210,15 +210,16 @@ def tile_moe_wsel_b_none_p_kernel(
             for j in range(HALVES):
                 first_product(0, j, c)
                 gate_and_round(0, j, c)
-        first_product(1, 0)
-        gate_and_round(1, 0)
+        for c in range(2):
+            first_product(1, 0, c)
+            gate_and_round(1, 0, c)
         for j in range(HALVES):
             turn(0, j)
             regroup(0, j)
             quantise_h(0, j)
-        for unit in ((1, 1), (2, 0)):
-            first_product(*unit)
-            gate_and_round(*unit)
+        for piece in ((1, 1, 0), (1, 1, 1), (2, 0)):
+            first_product(*piece)
+            gate_and_round(*piece)
         turn(1, 0)
         regroup(1, 0)
         first_product(2, 1)

@@ -28,6 +28,7 @@ LATE_H_AT = {(2, 0): 0, (1, 1): DEALT_AT + 2 * P}
 LATE_PLANE_AT = DEALT_AT + P
 LAST_W2_AT = DEALT_AT + 10 * P
 GATE_ROWS_AT = LAST_W2_AT + 4 * WIDTH
+W2_AT = GATE_ROWS_AT + 4 * P
 ON_VECTOR = ((1, 0, 1), (1, 1, 0))
 SUMS_BANK = {(0, 0, 0): 0, (0, 1, 0): 1, (0, 0, 1): 2, (0, 1, 1): 3, (1, 0, 0): 4, (1, 0, 1): 5, (1, 1, 0): 3, (1, 1, 1): 4, (2, 0): 0, (2, 1): 3}
 TURNED_BANK = {(0, 0): 0, (0, 1): 1, (1, 0): 1, (1, 1): 2, (2, 0): 0, (2, 1): 0}
@@ -75,7 +76,6 @@ def tile_moe_wsel_b_none_p_kernel(
         x_plane = held.tile([P, T], U8, name="x_plane", align_bytes=64)
         s2 = held.tile([P, G * WIDTH], U8, name="s2", align_bytes=64)
         w1_all = held.tile([P, COLUMNS], U32, name="w1_all", align_bytes=64)
-        w2_all = held.tile([P, COLUMNS], U32, name="w2_all", align_bytes=64)
 
         nc.vector.memset(s1_all[:].bitcast(I32), 0)
         nc.vector.memset(s2_all[:S2_ROW, :].bitcast(I32), 0)
@@ -90,18 +90,17 @@ def tile_moe_wsel_b_none_p_kernel(
         nc.sync.dma_start(list1[:], offs)
         load_scale_rows(nc, s1_all, w1_scales, 0)
         load_words(nc, w1_all, w1_words)
+        load_scale_rows(nc, x_plane, x_scales, X_ROW)
         gate_halves = gate.rearrange("r p (j c) -> (r p j) c", c=P)
         nc.sync.dma_start(out=gate_rows[: G * HALVES, :], in_=gate_halves[0 : G * HALVES * (P + 1) - P : P + 1, :])
         load_words(nc, x_codes, x_words)
-        load_scale_rows(nc, x_plane, x_scales, X_ROW)
-        load_words(nc, w2_all, w2_words)
 
         gate_bank = bank(Y_BANK[0][0], [P, P], "gate_bank")
         nc.tensor.transpose(gate_bank[:], gate_rows[:], identity[:])
         nc.scalar.activation(out=gate_cols[:], in_=gate_bank[:, : G * HALVES], func=COPY)
 
         s2_dealt = shared.tile([P, G * WIDTH], U8, name="s2_dealt", offset=DEALT_AT, align_bytes=64)
-        s2_spread = held.tile([P, G * WIDTH], U8, name="s2_spread", align_bytes=64)
+        s2_spread = shared.tile([P, G * WIDTH], U8, name="s2_spread", offset=W2_AT, align_bytes=64)
         parts = ((0, G - 1), (G - 1, G))
         for first, last in parts:
             gather(nc, s2_spread[:, first * WIDTH : last * WIDTH], s2_all, list2, first * WIDTH, (last - first) * WIDTH)
@@ -111,6 +110,8 @@ def tile_moe_wsel_b_none_p_kernel(
                 out=s2_dealt[:, chosen].rearrange("q (r d p) -> q d r p", r=last - first, d=4),
                 in_=s2_spread[:, chosen].rearrange("q (r p d) -> q d r p", r=last - first, d=4),
             )
+        w2_all = shared.tile([P, COLUMNS], U32, name="w2_all", offset=W2_AT, align_bytes=64)
+        load_words(nc, w2_all, w2_words)
         for v in range(4):
             nc.sync.dma_start(
                 out=s2[W2_ROW + v : P : 32, :].bitcast(I32), in_=s2_dealt[S2_ROW + v : P : 4, :].bitcast(I32)

from contextlib import ExitStack

import concourse.mybir as mybir
from concourse.masks import make_identity

F32 = mybir.dt.float32
BF16 = mybir.dt.bfloat16
I32 = mybir.dt.int32
U32 = mybir.dt.uint32
U16 = mybir.dt.uint16
U8 = mybir.dt.uint8
FP8X4 = mybir.dt.float8_e4m3fn_x4
COPY = mybir.ActivationFunctionType.Copy
MULT = mybir.AluOpType.mult

P = 128
T = 256
G = 3
WIDTH = 512
HALF = WIDTH // 2
COLUMNS = 3072
HALVES = T // P
PER_COLUMN = 16
X_ROW, W2_ROW = 8, 4
S2_ROW = P - 16
DEALT_AT = 7 * P
LATE_H_AT = {(2, 0): 0, (1, 1): DEALT_AT + 2 * P}
LATE_PLANE_AT = DEALT_AT + P
LAST_W2_AT = DEALT_AT + 10 * P
GATE_ROWS_AT = LAST_W2_AT + 4 * WIDTH
W2_AT = GATE_ROWS_AT + 4 * P
ON_VECTOR = ((1, 0, 1), (1, 1, 0))
SUMS_BANK = {(0, 0, 0): 0, (0, 1, 0): 1, (0, 0, 1): 2, (0, 1, 1): 3, (1, 0, 0): 4, (1, 0, 1): 5, (1, 1, 0): 3, (1, 1, 1): 4, (2, 0): 0, (2, 1): 3}
TURNED_BANK = {(0, 0): 0, (0, 1): 1, (1, 0): 1, (1, 1): 2, (2, 0): 0, (2, 1): 0}
Y_BANK = ((6, 4), (7, 5))

FLOPS = 2 * 2 * G * WIDTH * WIDTH * T


def gather(nc, out, window, offsets, first, count):
    nc.vector.tensor_copy(
        out=out, in_=window[:].indirect(offsets[:, first // PER_COLUMN : (first + count) // PER_COLUMN])
    )


def load_scale_rows(nc, plane, scales, first_row):
    rows = scales[0].bitcast(I32)
    for v in range(4):
        nc.sync.dma_start(out=plane[first_row + v : P : 32, :].bitcast(I32), in_=rows[v:16:4, :])


def load_words(nc, tile, words):
    nc.sync.dma_start(out=tile[:].bitcast(I32), in_=words[0].rearrange("p m d -> p (m d)").bitcast(I32))


def tile_moe_wsel_b_none_p_kernel(
    tc, x_words, x_scales, w1_words, w1_scales, w2_words, w2_scales, gate, offs, offs2, out_0, out_1, out_2
):
    nc = tc.nc
    with ExitStack() as ctx:
        held = ctx.enter_context(tc.tile_pool(name="held", bufs=1))
        shared = ctx.enter_context(tc.tile_pool(name="shared", bufs=1))
        psum = ctx.enter_context(tc.psum_pool(name="psum", bufs=1))

        def bank(number, shape, name):
            return psum.tile(shape, F32, name=name, tag="bank_%d" % number)

        list1 = held.tile([P, G * WIDTH // PER_COLUMN], U16, name="list1")
        list2 = held.tile([P, G * WIDTH // PER_COLUMN], U16, name="list2")
        x_codes = held.tile([P, T], U32, name="x_codes", align_bytes=64)
        gate_rows = shared.tile([P, P], F32, name="gate_rows", offset=GATE_ROWS_AT, align_bytes=64)
        gate_cols = held.tile([P, G * HALVES], F32, name="gate_cols")
        identity = held.tile([P, P], F32, name="identity")
        s1_all = held.tile([P, COLUMNS], U8, name="s1_all", align_bytes=64)
        s2_all = held.tile([P, COLUMNS], U8, name="s2_all", align_bytes=64)
        x_plane = held.tile([P, T], U8, name="x_plane", align_bytes=64)
        s2 = held.tile([P, G * WIDTH], U8, name="s2", align_bytes=64)
        w1_all = held.tile([P, COLUMNS], U32, name="w1_all", align_bytes=64)

        nc.vector.memset(s1_all[:].bitcast(I32), 0)
        nc.vector.memset(s2_all[:S2_ROW, :].bitcast(I32), 0)
        nc.vector.memset(x_plane[:].bitcast(I32), 0)
        nc.vector.memset(gate_rows[:], 0.0)
        nc.vector.memset(s2[:].bitcast(I32), 0)
        nc.vector.memset(identity[:], 0.0)
        make_identity(nc, identity[:], nomemset=True)

        nc.sync.dma_start(out=s2_all[S2_ROW:, :].bitcast(I32), in_=w2_scales[0].bitcast(I32))
        nc.sync.dma_start(list2[:], offs2)
        nc.sync.dma_start(list1[:], offs)
        load_scale_rows(nc, s1_all, w1_scales, 0)
        load_words(nc, w1_all, w1_words)
        load_scale_rows(nc, x_plane, x_scales, X_ROW)
        gate_halves = gate.rearrange("r p (j c) -> (r p j) c", c=P)
        nc.sync.dma_start(out=gate_rows[: G * HALVES, :], in_=gate_halves[0 : G * HALVES * (P + 1) - P : P + 1, :])
        load_words(nc, x_codes, x_words)

        gate_bank = bank(Y_BANK[0][0], [P, P], "gate_bank")
        nc.tensor.transpose(gate_bank[:], gate_rows[:], identity[:])
        nc.scalar.activation(out=gate_cols[:], in_=gate_bank[:, : G * HALVES], func=COPY)

        s2_dealt = shared.tile([P, G * WIDTH], U8, name="s2_dealt", offset=DEALT_AT, align_bytes=64)
        s2_spread = shared.tile([P, G * WIDTH], U8, name="s2_spread", offset=W2_AT, align_bytes=64)
        parts = ((0, G - 1), (G - 1, G))
        for first, last in parts:
            gather(nc, s2_spread[:, first * WIDTH : last * WIDTH], s2_all, list2, first * WIDTH, (last - first) * WIDTH)
        for first, last in parts:
            chosen = slice(first * WIDTH, last * WIDTH)
            nc.vector.tensor_copy(
                out=s2_dealt[:, chosen].rearrange("q (r d p) -> q d r p", r=last - first, d=4),
                in_=s2_spread[:, chosen].rearrange("q (r p d) -> q d r p", r=last - first, d=4),
            )
        w2_all = shared.tile([P, COLUMNS], U32, name="w2_all", offset=W2_AT, align_bytes=64)
        load_words(nc, w2_all, w2_words)
        for v in range(4):
            nc.sync.dma_start(
                out=s2[W2_ROW + v : P : 32, :].bitcast(I32), in_=s2_dealt[S2_ROW + v : P : 4, :].bitcast(I32)
            )
        s1_early = held.tile([P, (G - 1) * WIDTH], U8, name="s1_early", align_bytes=64)
        gather(nc, s1_early[:], s1_all, list1, 0, (G - 1) * WIDTH)
        w1 = held.tile([P, G * WIDTH], U32, name="w1", align_bytes=64)
        for first, count in ((0, HALF), (HALF, HALF), (WIDTH, WIDTH), (2 * WIDTH, WIDTH)):
            gather(nc, w1[:, first : first + count], w1_all, list1, first, count)
        s1_late = shared.tile([P, WIDTH], U8, name="s1_late", offset=GATE_ROWS_AT, align_bytes=64)
        gather(nc, s1_late[:], s1_all, list1, (G - 1) * WIDTH, WIDTH)

        units = [(r, j) for r in range(G) for j in range(HALVES)]
        h_rows = {unit: held.tile([P, 2, P, 2], BF16, name="h_rows_%d_%d" % unit) for unit in units}
        sums, turned, h_grouped, h_codes, h_plane = {}, {}, {}, {}, {}

        def columns(piece):
            return (piece[2] * HALF, HALF) if len(piece) == 3 else (0, WIDTH)

        def first_product(*piece):
            r, j = piece[:2]
            first, width = columns(piece)
            tokens = slice(j * P, (j + 1) * P)
            chosen = slice(r * WIDTH + first, r * WIDTH + first + width)
            sums[piece] = bank(SUMS_BANK[piece], [P, width], "sums")
            nc.tensor.matmul_mx(
                out=sums[piece][:],
                lhsT=x_codes[:, tokens].bitcast(FP8X4),
                lhsT_scale=x_plane[X_ROW:P, tokens],
                rhs=w1[:, chosen].bitcast(FP8X4),
                rhs_scale=s1_early[:, chosen] if r < G - 1 else s1_late[:],
                start=True,
                stop=True,
            )

        def gate_and_round(*piece):
            r, j = piece[:2]
            first, width = columns(piece)
            gate_column = gate_cols[:, HALVES * r + j : HALVES * r + j + 1]
            part = h_rows[r, j][:, :, first // 4 : (first + width) // 4, :]
            dealt = sums[piece][:].rearrange("t (p u e) -> t u p e", u=2, e=2)
            if piece in ON_VECTOR:
                nc.vector.tensor_scalar(out=part, in0=dealt, scalar1=gate_column, scalar2=None, op0=MULT)
            else:
                nc.scalar.activation(out=part, in_=dealt, func=COPY, scale=gate_column)

        def turn(*unit):
            pairs = h_rows[unit][:].rearrange("t u p e -> t (u p e)").bitcast(F32)
            turned[unit] = bank(TURNED_BANK[unit], [P, 2, P], "turned")
            for u in range(2):
                nc.tensor.transpose(turned[unit][:, u, :], pairs[:, u * P : (u + 1) * P], identity[:])

        def regroup(*unit):
            name = "h_grouped_%d_%d" % unit
            if unit in LATE_H_AT:
                h_grouped[unit] = shared.tile([P, P * 4], BF16, name=name, offset=LATE_H_AT[unit], align_bytes=64)
            else:
                h_grouped[unit] = held.tile([P, P * 4], BF16, name=name, align_bytes=64)
            nc.scalar.copy(
                out=h_grouped[unit][:].bitcast(F32).rearrange("p (t u) -> p t u", u=2),
                in_=turned[unit][:].rearrange("p u t -> p t u"),
            )

        def quantise_h(*unit):
            h_codes[unit] = held.tile([P, P], U32, name="h_codes_%d_%d" % unit, align_bytes=64)
            name = "h_plane_%d_%d" % unit
            if unit == (1, 0):
                h_plane[unit] = shared.tile([P, P], U8, name=name, offset=LATE_PLANE_AT, align_bytes=64)
            else:
                h_plane[unit] = held.tile([P, P], U8, name=name, align_bytes=64)
            nc.vector.quantize_mx(out=h_codes[unit][:].bitcast(FP8X4), scales=h_plane[unit][:], in_=h_grouped[unit][:])

        w2 = {}

        def gather_w2(r):
            if r < G - 1:
                w2[r] = held.tile([P, WIDTH], U32, name="w2_%d" % r, align_bytes=64)
            else:
                w2[r] = shared.tile([P, WIDTH], U32, name="w2_%d" % r, offset=LAST_W2_AT, align_bytes=64)
            gather(nc, w2[r][:].rearrange("q (d p) -> q p d", d=4), w2_all, list2, r * WIDTH, WIDTH)

        y_sums = [[bank(Y_BANK[j][pair], [P, 2, P], "y_sums") for pair in range(2)] for j in range(HALVES)]

        def second_product(r, j):
            for d in range(4):
                nc.tensor.matmul_mx(
                    out=y_sums[j][d // 2][:, d % 2, :],
                    lhsT=w2[r][:, d * P : (d + 1) * P].bitcast(FP8X4),
                    lhsT_scale=s2[W2_ROW:P, r * WIDTH + d * P : r * WIDTH + (d + 1) * P],
                    rhs=h_codes[r, j][:].bitcast(FP8X4),
                    rhs_scale=h_plane[r, j][:],
                    start=(r == 0 and d % 2 == 0),
                    stop=(r == G - 1 and d % 2 == 1),
                )

        for c in range(2):
            for j in range(HALVES):
                first_product(0, j, c)
                gate_and_round(0, j, c)
        for c in range(2):
            first_product(1, 0, c)
            gate_and_round(1, 0, c)
        for j in range(HALVES):
            turn(0, j)
            regroup(0, j)
            quantise_h(0, j)
        for piece in ((1, 1, 0), (1, 1, 1), (2, 0)):
            first_product(*piece)
            gate_and_round(*piece)
        turn(1, 0)
        regroup(1, 0)
        first_product(2, 1)
        gate_and_round(2, 1)
        turn(1, 1)
        turn(2, 0)
        regroup(2, 0)
        regroup(1, 1)
        gather_w2(0)
        gather_w2(1)
        for j in range(HALVES):
            second_product(0, j)
        turn(2, 1)
        regroup(2, 1)
        quantise_h(1, 0)
        second_product(1, 0)
        gather_w2(2)
        for unit in ((2, 0), (1, 1), (2, 1)):
            quantise_h(*unit)
            second_product(*unit)

        out_rows = out_0.rearrange("(p d) t -> p d t", d=4)
        out_words = out_1[0].rearrange("p t d -> p (t d)").bitcast(I32)
        y = [held.tile([P, 4, P], F32, name="y_%d" % j) for j in range(HALVES)]
        y_grouped = [held.tile([P, P, 4], BF16, name="y_grouped_%d" % j, align_bytes=64) for j in range(HALVES)]
        y_codes = held.tile([P, T], U32, name="y_codes", align_bytes=64)
        y_plane = held.tile([P, T], U8, name="y_plane", align_bytes=64)

        def leave_psum(j):
            nc.scalar.copy(out=y[j][:, :2, :], in_=y_sums[j][0][:])
            if j == 0:
                nc.vector.tensor_copy(out=y[j][:, 2:, :], in_=y_sums[j][1][:])
            else:
                nc.scalar.copy(out=y[j][:, 2:, :], in_=y_sums[j][1][:])
            nc.sync.dma_start(out=out_rows[:, :, j * P : (j + 1) * P], in_=y[j][:])

        def round_y(j):
            nc.vector.tensor_copy(out=y_grouped[j][:], in_=y[j][:].rearrange("p d t -> p t d"))

        def quantise_y(j):
            tokens = slice(j * P, (j + 1) * P)
            nc.vector.quantize_mx(
                out=y_codes[:, tokens].bitcast(FP8X4),
                scales=y_plane[:, tokens],
                in_=y_grouped[j][:].rearrange("p t d -> p (t d)"),
            )

        for j in range(HALVES):
            leave_psum(j)
            round_y(j)
        for j in range(HALVES):
            quantise_y(j)
        nc.sync.dma_start(out=out_words, in_=y_codes[:].bitcast(I32))
        scale_rows = out_2[0].bitcast(I32)
        for v in range(4):
            queue = nc.scalar if v < 2 else nc.sync
            queue.dma_start(out=scale_rows[v:16:4, :], in_=y_plane[v:P:32, :].bitcast(I32))
